import numpy as np
import ml_dtypes


def mxq(x, axis, fmt="e4m3"):
    dtype, down = {"e4m3": (ml_dtypes.float8_e4m3fn, 7), "e5m2": (ml_dtypes.float8_e5m2, 14)}[fmt]
    v = np.moveaxis(np.asarray(x, np.float32).astype(ml_dtypes.bfloat16).astype(np.float64), axis, -1)
    blocks = v.reshape(v.shape[:-1] + (-1, 32))
    amax = np.abs(blocks).max(-1, keepdims=True)
    byte = np.maximum(np.where(amax > 0, np.frexp(amax)[1] - 1 + 127, 0) - down, 1)
    scale = np.exp2(byte - 127.0)
    codes = (blocks / scale).astype(np.float32).astype(dtype).astype(np.float64)
    return np.moveaxis((codes * scale).reshape(v.shape), -1, axis)


WIDE = False


def mx_kscale(k):
    if not WIDE:
        return np.ones(k)
    levels = np.array([10, -10, 5, -5, 0])
    if k % 512:
        return np.exp2(np.random.permutation(np.resize(levels, k // 32))).repeat(32)
    a = np.empty((k // 512, 16))
    for p in range(k // 512):
        a[p, :8] = np.random.permutation(np.resize(levels, 8))
        for g in range(8):
            far = levels[np.abs(levels - a[p, g]) >= 10]
            a[p, g + 8] = far[np.random.randint(len(far))]
    return np.exp2(a.ravel()).repeat(32)


def f64(x):
    return np.asarray(x).astype(np.float64)


def striped(idx):
    return np.tile(np.asarray(idx).reshape(-1, 16).T, (8, 1)).astype(np.uint16)


def unstriped(offs):
    return offs[:16].T.reshape(-1).astype(np.int64)


E2M1 = np.array([0.0, 0.5, 1.0, 1.5, 2.0, 3.0, 4.0, 6.0, -0.0, -0.5, -1.0, -1.5, -2.0, -3.0, -4.0, -6.0])


def pack_weight(w, fmt):
    k, n = w.shape
    w = f64(np.asarray(w, np.float32).astype(ml_dtypes.bfloat16)).reshape(k // 32, 32, n)
    amax = np.abs(w).max(1)
    if fmt == "e4m3":
        byte = np.frexp(amax)[1] - 1 + 127 - 7
    else:
        mant, ex = np.frexp(amax / 6.0)
        byte = np.where(mant > 0.5, ex, ex - 1) + 127
    byte = np.clip(np.where(amax > 0, byte, 1), 1, 254)
    scaled = (w * np.exp2(127.0 - byte)[:, None, :]).reshape(k, n).astype(np.float32)
    by_word = np.ascontiguousarray(scaled.reshape(k // 512, 128, 4, n).transpose(0, 1, 3, 2))
    if fmt == "e4m3":
        words = by_word.astype(ml_dtypes.float8_e4m3fn).view(np.uint8)
    else:
        c = by_word.astype(ml_dtypes.float4_e2m1fn).view(np.uint8) & 0xF
        words = (c[..., 0::2] | (c[..., 1::2] << 4)).reshape(k // 512, 128, 2 * n)
    return np.ascontiguousarray(words), np.ascontiguousarray(byte.astype(np.uint8).reshape(k // 512, 16, n))


def unpack_weight(words, scales, fmt):
    g, _, n = scales.shape
    words = np.ascontiguousarray(words).reshape(g, 128, n, -1)
    if fmt == "e4m3":
        vals = words.view(ml_dtypes.float8_e4m3fn).astype(np.float64)
    else:
        nib = np.empty((g, 128, n, 4), np.uint8)
        nib[..., 0::2] = words & 0xF
        nib[..., 1::2] = words >> 4
        vals = E2M1[nib]
    vals = vals * np.repeat(np.exp2(scales.astype(np.float64) - 127.0), 8, axis=1)[..., None]
    return vals.transpose(0, 1, 3, 2).reshape(g * 512, n)


K, U, R, T, I, F = 512, 1024, 512, 2048, 512, 512


def setup_inputs():
    n = np.random.standard_normal
    idx = np.random.randint(0, U, I)
    idx2 = np.random.randint(0, U, I)
    idx3 = np.random.randint(0, U, I)
    idx4 = np.random.permutation(T)[:I]
    fk = mx_kscale(K)
    fr = mx_kscale(R)
    skipp = pack_weight(n((R, T)) / fr[:, None], "e2m1")
    return {
        "coarse": (n((K, U)) / fk[:, None]).astype(np.float32),
        "wa": (np.random.uniform(0.4, 0.7, (1, I))).astype(np.float32),
        "wb": (np.random.uniform(0.2, 0.4, (1, I))).astype(np.float32),
        "wc": (np.random.uniform(0.1, 0.3, (1, I))).astype(np.float32),
        "wf": (n((K, F)) * 1 / np.sqrt(K) * fk[:, None]).astype(np.float32),
        "skip_words": skipp[0],
        "skip_scales": skipp[1],
        "ws": (n((R, F)) * 0.7 / np.sqrt(R) * fr[:, None]).astype(np.float32),
        "bias": (0.3 * n((F, 1))).astype(np.float32),
        "offs": striped(idx),
        "offs2": striped(idx2),
        "offs3": striped(idx3),
        "offs4": striped(idx4),
    }


def reference(coarse, wa, wb, wc, wf, skip_words, skip_scales, ws, bias, offs, offs2, offs3, offs4):
    idx = unstriped(offs)
    idx2 = unstriped(offs2)
    idx3 = unstriped(offs3)
    idx4 = unstriped(offs4)
    skipu = unpack_weight(skip_words, skip_scales, "e2m1")
    x = f64(coarse)[:, idx] * f64(wa) + f64(coarse)[:, idx2] * f64(wb) + f64(coarse)[:, idx3] * f64(wc)
    wfq = mxq(f64(wf), 0, "e4m3")
    xq = mxq(x, 0, "e4m3")
    wsq = mxq(f64(ws), 0, "e4m3")
    skipidx4g = skipu[:, idx4]
    z = wfq.T @ xq + wsq.T @ skipidx4g
    y = np.maximum(z + f64(bias), 0.0)
    return y

@@ -1,0 +1,188 @@
+from contextlib import ExitStack
+
+import concourse.mybir as mybir
+from concourse.masks import make_identity
+
+F32 = mybir.dt.float32
+BF16 = mybir.dt.bfloat16
+I32 = mybir.dt.int32
+U32 = mybir.dt.uint32
+U16 = mybir.dt.uint16
+U8 = mybir.dt.uint8
+FP8X4 = mybir.dt.float8_e4m3fn_x4
+FP4X4 = mybir.dt.float4_e2m1fn_x4
+ACT = mybir.ActivationFunctionType
+ALU = mybir.AluOpType
+
+P = 128
+K, U, R, T, NI, F = 512, 1024, 512, 2048, 512, 512
+FLOPS = 2 * (K + R) * NI * F
+
+
+def tile_attend_threenn_kernel(tc, coarse, wa, wb, wc, wf, skip_words, skip_scales, ws, bias,
+                                offs, offs2, offs3, offs4, out):
+    nc = tc.nc
+    with ExitStack() as ctx:
+        keep = ctx.enter_context(tc.tile_pool(name="keep", bufs=1))
+        ring = ctx.enter_context(tc.tile_pool(name="ring", bufs=4))
+        psum = ctx.enter_context(tc.psum_pool(name="psum", bufs=1))
+
+        def bank(b):
+            return psum.tile([P, 512], F32, name="bank%d" % b)
+
+        lists = [keep.tile([P, NI // 16], U16, name="list%d" % l) for l in range(4)]
+        planes = [keep.tile([P, U], F32, name="plane%d" % t) for t in range(4)]
+        rows = keep.tile([P, P], F32, name="rows")
+        cols = keep.tile([P, 16], F32, name="cols")
+        ident = keep.tile([P, P], F32, name="ident")
+        sk_w = keep.tile([P, T], U16, name="sk_w")
+        sk_s = keep.tile([P, T], U8, name="sk_s")
+        raw = {}
+        grp = {}
+        codes = {}
+        scal = {}
+        for n in ("wf", "ws"):
+            raw[n] = [keep.tile([P, 4, F // 2], F32, name="raw_%s%d" % (n, h)) for h in range(2)]
+            grp[n] = keep.tile([P, F, 4], BF16, name="grp_" + n, align_bytes=64)
+            codes[n] = keep.tile([P, F], U32, name="codes_" + n, align_bytes=64)
+            scal[n] = keep.tile([P, F], U8, name="scal_" + n, align_bytes=64)
+
+        nc.gpsimd.memset(rows[:], 0.0)
+        make_identity(nc, ident[:])
+        nc.gpsimd.memset(sk_s[:].bitcast(I32), 0)
+
+        cview = coarse.rearrange("(p t) u -> p t u", t=4)
+        wview = {"wf": wf.rearrange("(p t) f -> p t f", t=4), "ws": ws.rearrange("(p t) f -> p t f", t=4)}
+
+        for l, w in enumerate((wa, wb, wc)):
+            nc.scalar.dma_start(out=rows[4 * l:4 * l + 4, :], in_=w.rearrange("o (c p) -> (o c) p", p=P))
+        nc.scalar.dma_start(out=rows[12:16, :], in_=bias.rearrange("(j p) o -> j (p o)", p=P))
+
+        def load_w(n, h):
+            nc.sync.dma_start(out=raw[n][h][:], in_=wview[n][:, :, 256 * h:256 * (h + 1)])
+
+        nc.sync.dma_start(lists[0][:], offs)
+        nc.sync.dma_start(out=planes[0][:], in_=cview[:, 0, :])
+        nc.sync.dma_start(lists[1][:], offs2)
+        nc.sync.dma_start(lists[2][:], offs3)
+        nc.sync.dma_start(out=planes[1][:], in_=cview[:, 1, :])
+        load_w("wf", 0)
+        nc.sync.dma_start(out=planes[2][:], in_=cview[:, 2, :])
+        load_w("wf", 1)
+        nc.sync.dma_start(out=planes[3][:], in_=cview[:, 3, :])
+        nc.sync.dma_start(lists[3][:], offs4)
+        nc.sync.dma_start(out=sk_w[:].bitcast(I32), in_=skip_words[0].bitcast(I32))
+        for q in range(4):
+            nc.sync.dma_start(out=sk_s[:].bitcast(I32)[32 * q:32 * q + 4, :],
+                              in_=skip_scales[0].bitcast(I32)[4 * q:4 * q + 4, :])
+        load_w("ws", 0)
+        load_w("ws", 1)
+
+        b = bank(7)
+        nc.tensor.transpose(b[:, 0:P], rows[:], ident[:])
+        nc.scalar.copy(out=cols[:], in_=b[:, 0:16])
+
+        def interleave(n, j):
+            src = raw[n][j // 2][:, :, P * (j % 2):P * (j % 2 + 1)].rearrange("p t (c i) -> p c t i", i=4)
+            dst = grp[n][:, P * j:P * (j + 1), :].rearrange("p (c i) t -> p c t i", i=4)
+            nc.scalar.copy(out=dst, in_=src)
+
+        def quant_w(n):
+            nc.vector.quantize_mx(out=codes[n][:].bitcast(FP8X4), scales=scal[n][:],
+                                  in_=grp[n][:].rearrange("p f t -> p (f t)"))
+
+        fwd_count = [0]
+
+        def unit(t, l, c0, nch, xacc, tag=None):
+            n = P * nch
+            if tag is None:
+                g = ring.tile([P, n], F32, name="g", align_bytes=64)
+            else:
+                g = keep.tile([P, n], F32, name=tag, align_bytes=64)
+            nc.vector.tensor_copy(g[:], planes[t][:].indirect(lists[l][:, 8 * c0:8 * (c0 + nch)]))
+            fb = bank(fwd_count[0] % 3)
+            fwd_count[0] = fwd_count[0] + 1
+            s = ring.tile([P, n], F32, name="s")
+            for c in range(nch):
+                nc.tensor.transpose(fb[:, P * c:P * (c + 1)], g[:, P * c:P * (c + 1)], ident[:])
+            for c in range(nch):
+                nc.scalar.activation(out=s[:, P * c:P * (c + 1)], in_=fb[:, P * c:P * (c + 1)], func=ACT.Copy,
+                                     scale=cols[:, 4 * l + c0 + c:4 * l + c0 + c + 1])
+            for c in range(nch):
+                nc.tensor.matmul(xacc[c][:, P * t:P * (t + 1)], s[:, P * c:P * (c + 1)], ident[:],
+                                 start=(l == 0), stop=(l == 2), is_transpose=True)
+
+        def finish_x(name, nch, xacc):
+            xg = keep.tile([P, P * nch, 4], BF16, name="xg" + name, align_bytes=64)
+            xc = keep.tile([P, P * nch], U32, name="xc" + name, align_bytes=64)
+            xs = keep.tile([P, P * nch], U8, name="xs" + name, align_bytes=64)
+            for c in range(nch):
+                nc.scalar.copy(out=xg[:, P * c:P * (c + 1), :], in_=xacc[c][:].rearrange("p (t i) -> p i t", t=4))
+            nc.vector.quantize_mx(out=xc[:].bitcast(FP8X4), scales=xs[:], in_=xg[:].rearrange("p i t -> p (i t)"))
+            return xc, xs
+
+        def gather_skip(h, tag_w, tag_s):
+            gw = keep.tile([P, 256], U16, name=tag_w, align_bytes=64)
+            gs = keep.tile([P, 256], U8, name=tag_s, align_bytes=64)
+            nc.vector.tensor_copy(gw[:], sk_w[:].indirect(lists[3][:, 16 * h:16 * (h + 1)]))
+            nc.vector.tensor_copy(gs[:], sk_s[:].indirect(lists[3][:, 16 * h:16 * (h + 1)]))
+            return gw, gs
+
+        def products(dst, j, xq, xo, sq, so):
+            fc = slice(P * j, P * (j + 1))
+            nc.tensor.matmul_mx(out=dst, lhsT=codes["wf"][:, fc].bitcast(FP8X4), lhsT_scale=scal["wf"][:, fc],
+                                rhs=xq[0][:, xo:xo + P].bitcast(FP8X4), rhs_scale=xq[1][:, xo:xo + P],
+                                start=True, stop=False)
+            nc.tensor.matmul_mx(out=dst, lhsT=codes["ws"][:, fc].bitcast(FP8X4), lhsT_scale=scal["ws"][:, fc],
+                                rhs=sq[0][:, so:so + P].bitcast(FP4X4), rhs_scale=sq[1][:, so:so + P],
+                                start=False, stop=True)
+
+        def relu(eng, dst, src, j):
+            bcol = cols[:, 12 + j:13 + j]
+            if eng == "s":
+                nc.scalar.activation(out=dst, in_=src, func=ACT.Relu, bias=bcol)
+            else:
+                nc.vector.tensor_scalar(out=dst, in0=src, scalar1=bcol, scalar2=0.0, op0=ALU.add, op1=ALU.max)
+
+        oview = out.rearrange("(j p) i -> p j i", p=P)
+
+        xa = [bank(3), bank(4)]
+        for t in range(4):
+            for l in range(3):
+                unit(t, l, 0, 2, xa)
+                n = 3 * t + l
+                if n in (4, 6, 8, 10):
+                    interleave("wf", (n - 4) // 2)
+        quant_w("wf")
+        xqa = finish_x("a", 2, xa)
+        sq0 = gather_skip(0, "gw0", "gs0")
+        xb = [bank(5)]
+        for t in range(4):
+            for l in range(3):
+                unit(t, l, 2, 1, xb)
+            interleave("ws", t)
+        quant_w("ws")
+        xqb = finish_x("b", 1, xb)
+        oa = keep.tile([P, 4, 256], F32, name="oa")
+        xc_ = [bank(3)]
+        for t in range(4):
+            for l in range(3):
+                unit(t, l, 3, 1, xc_, tag={(3, 0): "hold0", (3, 1): "hold1"}.get((t, l)))
+            if t < 2:
+                ob = bank(6 + t)
+                for jj in range(2):
+                    for c in range(2):
+                        products(ob[:, 256 * jj + P * c:256 * jj + P * (c + 1)], 2 * t + jj, xqa, P * c, sq0, P * c)
+                for jj in range(2):
+                    relu("s", oa[:, 2 * t + jj, :], ob[:, 256 * jj:256 * (jj + 1)], 2 * t + jj)
+                nc.sync.dma_start(out=oview[:, 2 * t:2 * t + 2, 0:256], in_=oa[:, 2 * t:2 * t + 2, :])
+        sq1 = gather_skip(1, "hold0", "hold1")
+        xqc = finish_x("c", 1, xc_)
+        obc = keep.tile([P, 4, 256], F32, name="obc")
+        for j in range(4):
+            ob = bank(4 + j)
+            products(ob[:, 0:P], j, xqb, 0, sq1, 0)
+            products(ob[:, P:2 * P], j, xqc, 0, sq1, P)
+            relu("sv"[j % 2], obc[:, j, :], ob[:, 0:256], j)
+            if j % 2 == 1:
+                nc.sync.dma_start(out=oview[:, j - 1:j + 1, 256:512], in_=obc[:, j - 1:j + 1, :])

@@ -24,7 +24,7 @@ def tile_attend_threenn_kernel(tc, coarse, wa, wb, wc, wf, skip_words, skip_scal
     nc = tc.nc
     with ExitStack() as ctx:
         keep = ctx.enter_context(tc.tile_pool(name="keep", bufs=1))
-        ring = ctx.enter_context(tc.tile_pool(name="ring", bufs=4))
+        ring = ctx.enter_context(tc.tile_pool(name="ring", bufs=6))
         psum = ctx.enter_context(tc.psum_pool(name="psum", bufs=1))
 
         def bank(b):
@@ -32,8 +32,8 @@ def tile_attend_threenn_kernel(tc, coarse, wa, wb, wc, wf, skip_words, skip_scal
 
         lists = [keep.tile([P, NI // 16], U16, name="list%d" % l) for l in range(4)]
         planes = [keep.tile([P, U], F32, name="plane%d" % t) for t in range(4)]
-        rows = keep.tile([P, P], F32, name="rows")
-        cols = keep.tile([P, 16], F32, name="cols")
+        wcol = [keep.tile([P, 4], F32, name="wcol%d" % l) for l in range(3)]
+        bcol = keep.tile([P, 4], F32, name="bcol")
         ident = keep.tile([P, P], F32, name="ident")
         sk_w = keep.tile([P, T], U16, name="sk_w")
         sk_s = keep.tile([P, T], U8, name="sk_s")
@@ -42,45 +42,50 @@ def tile_attend_threenn_kernel(tc, coarse, wa, wb, wc, wf, skip_words, skip_scal
         codes = {}
         scal = {}
         for n in ("wf", "ws"):
-            raw[n] = [keep.tile([P, 4, F // 2], F32, name="raw_%s%d" % (n, h)) for h in range(2)]
-            grp[n] = keep.tile([P, F, 4], BF16, name="grp_" + n, align_bytes=64)
+            raw[n] = [keep.tile([P, 4, F // 2], F32, name="raw_%s%d" % (n, h), align_bytes=64) for h in range(2)]
             codes[n] = keep.tile([P, F], U32, name="codes_" + n, align_bytes=64)
             scal[n] = keep.tile([P, F], U8, name="scal_" + n, align_bytes=64)
 
-        nc.gpsimd.memset(rows[:], 0.0)
+        wbc = [keep.tile([P, NI], F32, name="wbc%d" % l) for l in range(3)]
         make_identity(nc, ident[:])
-        nc.gpsimd.memset(sk_s[:].bitcast(I32), 0)
+        nc.vector.memset(sk_s[:].bitcast(I32), 0)
 
         cview = coarse.rearrange("(p t) u -> p t u", t=4)
         wview = {"wf": wf.rearrange("(p t) f -> p t f", t=4), "ws": ws.rearrange("(p t) f -> p t f", t=4)}
 
-        for l, w in enumerate((wa, wb, wc)):
-            nc.scalar.dma_start(out=rows[4 * l:4 * l + 4, :], in_=w.rearrange("o (c p) -> (o c) p", p=P))
-        nc.scalar.dma_start(out=rows[12:16, :], in_=bias.rearrange("(j p) o -> j (p o)", p=P))
+        def load_col(l):
+            nc.sync.dma_start(out=wcol[l][:], in_=(wa, wb, wc)[l].rearrange("o (p c) -> p (o c)", c=4))
 
         def load_w(n, h):
             nc.sync.dma_start(out=raw[n][h][:], in_=wview[n][:, :, 256 * h:256 * (h + 1)])
 
+        load_col(0)
         nc.sync.dma_start(lists[0][:], offs)
         nc.sync.dma_start(out=planes[0][:], in_=cview[:, 0, :])
+        load_col(1)
         nc.sync.dma_start(lists[1][:], offs2)
+        load_col(2)
         nc.sync.dma_start(lists[2][:], offs3)
-        nc.sync.dma_start(out=planes[1][:], in_=cview[:, 1, :])
         load_w("wf", 0)
-        nc.sync.dma_start(out=planes[2][:], in_=cview[:, 2, :])
+        nc.sync.dma_start(out=planes[1][:], in_=cview[:, 1, :])
         load_w("wf", 1)
+        nc.sync.dma_start(out=planes[2][:], in_=cview[:, 2, :])
+        load_w("ws", 0)
+        load_w("ws", 1)
         nc.sync.dma_start(out=planes[3][:], in_=cview[:, 3, :])
         nc.sync.dma_start(lists[3][:], offs4)
         nc.sync.dma_start(out=sk_w[:].bitcast(I32), in_=skip_words[0].bitcast(I32))
         for q in range(4):
             nc.sync.dma_start(out=sk_s[:].bitcast(I32)[32 * q:32 * q + 4, :],
                               in_=skip_scales[0].bitcast(I32)[4 * q:4 * q + 4, :])
-        load_w("ws", 0)
-        load_w("ws", 1)
+        with nc.allow_non_contiguous_dma(reason="one bias value a partition"):
+            nc.sync.dma_start(out=bcol[:], in_=bias.rearrange("(j p) o -> p (j o)", p=P))
 
-        b = bank(7)
-        nc.tensor.transpose(b[:, 0:P], rows[:], ident[:])
-        nc.scalar.copy(out=cols[:], in_=b[:, 0:16])
+        for l in range(3):
+            b = bank(5 + l)
+            for c in range(4):
+                nc.tensor.transpose(b[:, P * c:P * (c + 1)], wcol[l][:, c:c + 1].to_broadcast([P, P]), ident[:])
+            nc.scalar.copy(out=wbc[l][:].rearrange("p (n c) -> p n c", c=4), in_=b[:].rearrange("p (c n) -> p n c", c=4))
 
         def interleave(n, j):
             src = raw[n][j // 2][:, :, P * (j % 2):P * (j % 2 + 1)].rearrange("p t (c i) -> p c t i", i=4)
@@ -91,35 +96,36 @@ def tile_attend_threenn_kernel(tc, coarse, wa, wb, wc, wf, skip_words, skip_scal
             nc.vector.quantize_mx(out=codes[n][:].bitcast(FP8X4), scales=scal[n][:],
                                   in_=grp[n][:].rearrange("p f t -> p (f t)"))
 
-        fwd_count = [0]
-
-        def unit(t, l, c0, nch, xacc, tag=None):
+        def unit(t, l, c0, nch, ydst, tag=None):
             n = P * nch
-            if tag is None:
-                g = ring.tile([P, n], F32, name="g", align_bytes=64)
-            else:
-                g = keep.tile([P, n], F32, name=tag, align_bytes=64)
-            nc.vector.tensor_copy(g[:], planes[t][:].indirect(lists[l][:, 8 * c0:8 * (c0 + nch)]))
-            fb = bank(fwd_count[0] % 3)
-            fwd_count[0] = fwd_count[0] + 1
-            s = ring.tile([P, n], F32, name="s")
-            for c in range(nch):
-                nc.tensor.transpose(fb[:, P * c:P * (c + 1)], g[:, P * c:P * (c + 1)], ident[:])
-            for c in range(nch):
-                nc.scalar.activation(out=s[:, P * c:P * (c + 1)], in_=fb[:, P * c:P * (c + 1)], func=ACT.Copy,
-                                     scale=cols[:, 4 * l + c0 + c:4 * l + c0 + c + 1])
-            for c in range(nch):
-                nc.tensor.matmul(xacc[c][:, P * t:P * (t + 1)], s[:, P * c:P * (c + 1)], ident[:],
-                                 start=(l == 0), stop=(l == 2), is_transpose=True)
+            slot = (3 * t + l) % 6
+            g = keep.tile([P, n], F32, name=tag or "g%d" % slot, align_bytes=64)
+            nc.vector.tensor_tensor(g[:], planes[t][:].indirect(lists[l][:, 8 * c0:8 * (c0 + nch)]),
+                                    wbc[l][:, P * c0:P * (c0 + nch)], ALU.mult)
+            return g
 
-        def finish_x(name, nch, xacc):
-            xg = keep.tile([P, P * nch, 4], BF16, name="xg" + name, align_bytes=64)
-            xc = keep.tile([P, P * nch], U32, name="xc" + name, align_bytes=64)
-            xs = keep.tile([P, P * nch], U8, name="xs" + name, align_bytes=64)
+        def turn(y, nch, u, z, name):
+            xb = ring.tile([P, nch, P, 2], BF16, name="xb", align_bytes=64)
+            nc.scalar.copy(out=xb[:], in_=y[:, 0:256 * nch].rearrange("i (c e p) -> i c p e", c=nch, e=2))
+            words = xb[:].rearrange("i c p e -> i (c p e)").bitcast(F32)
             for c in range(nch):
-                nc.scalar.copy(out=xg[:, P * c:P * (c + 1), :], in_=xacc[c][:].rearrange("p (t i) -> p i t", t=4))
-            nc.vector.quantize_mx(out=xc[:].bitcast(FP8X4), scales=xs[:], in_=xg[:].rearrange("p i t -> p (i t)"))
+                nc.tensor.transpose(z[:, 256 * c + P * u:256 * c + P * (u + 1)], words[:, P * c:P * (c + 1)], ident[:])
+
+        def finish_x(name, nch, z, tag=None):
+            xg = keep.tile([P, P * nch * 4], BF16, name="xg" + name, align_bytes=64)
+            xc = keep.tile([P, P * nch], U32, name=tag or "xc" + name, align_bytes=64)
+            xs = keep.tile([P, P * nch], U8, name="xs" + name, align_bytes=64)
+            nc.scalar.copy(out=xg[:].bitcast(F32).rearrange("p (c i u) -> p c i u", c=nch, u=2),
+                           in_=z[:, 0:256 * nch].rearrange("p (c u i) -> p c i u", c=nch, u=2))
+            nc.vector.quantize_mx(out=xc[:].bitcast(FP8X4), scales=xs[:], in_=xg[:])
             return xc, xs
+
+        def plane(t, c0, nch, ydst, tags={}):
+            gs = [unit(t, l, c0, nch, ydst, tags.get(l)) for l in range(3)]
+            for c in range(nch):
+                for l in range(3):
+                    nc.tensor.matmul(ydst[c], gs[l][:, P * c:P * (c + 1)], ident[:],
+                                     start=(l == 0), stop=(l == 2), is_transpose=True)
 
         def gather_skip(h, tag_w, tag_s):
             gw = keep.tile([P, 256], U16, name=tag_w, align_bytes=64)
@@ -138,51 +144,64 @@ def tile_attend_threenn_kernel(tc, coarse, wa, wb, wc, wf, skip_words, skip_scal
                                 start=False, stop=True)
 
         def relu(eng, dst, src, j):
-            bcol = cols[:, 12 + j:13 + j]
+            bj = bcol[:, j:j + 1]
             if eng == "s":
-                nc.scalar.activation(out=dst, in_=src, func=ACT.Relu, bias=bcol)
+                nc.scalar.activation(out=dst, in_=src, func=ACT.Relu, bias=bj)
             else:
-                nc.vector.tensor_scalar(out=dst, in0=src, scalar1=bcol, scalar2=0.0, op0=ALU.add, op1=ALU.max)
+                nc.vector.tensor_scalar(out=dst, in0=src, scalar1=bj, scalar2=0.0, op0=ALU.add, op1=ALU.max)
 
         oview = out.rearrange("(j p) i -> p j i", p=P)
 
-        xa = [bank(3), bank(4)]
-        for t in range(4):
-            for l in range(3):
-                unit(t, l, 0, 2, xa)
-                n = 3 * t + l
-                if n in (4, 6, 8, 10):
-                    interleave("wf", (n - 4) // 2)
-        quant_w("wf")
-        xqa = finish_x("a", 2, xa)
+        def chunk(c0, nch, ybanks, z, tags={}, after={}):
+            for u in range(2):
+                y = bank(ybanks[u])
+                for e in range(2):
+                    t = 2 * u + e
+                    plane(t, c0, nch, [y[:, 256 * c + P * e:256 * c + P * (e + 1)] for c in range(nch)],
+                          {l: tags[(t, l)] for l in range(3) if (t, l) in tags})
+                turn(y, nch, u, z, "")
+                if u in after:
+                    after[u]()
+
+        def prep(n):
+            grp[n] = keep.tile([P, F, 4], BF16, name="grp_" + n, align_bytes=64)
+            for j in range(4):
+                interleave(n, j)
+            quant_w(n)
+
+        za = bank(4)
+        chunk(0, 2, (0, 1), za, {(0, 2): "grp_wf"})
+        prep("wf")
+        prep("ws")
         sq0 = gather_skip(0, "gw0", "gs0")
-        xb = [bank(5)]
-        for t in range(4):
-            for l in range(3):
-                unit(t, l, 2, 1, xb)
-            interleave("ws", t)
-        quant_w("ws")
-        xqb = finish_x("b", 1, xb)
+        xqa = finish_x("a", 2, za)
+        zb = bank(5)
+        chunk(2, 1, (2, 3), zb)
         oa = keep.tile([P, 4, 256], F32, name="oa")
-        xc_ = [bank(3)]
-        for t in range(4):
-            for l in range(3):
-                unit(t, l, 3, 1, xc_, tag={(3, 0): "hold0", (3, 1): "hold1"}.get((t, l)))
-            if t < 2:
-                ob = bank(6 + t)
-                for jj in range(2):
-                    for c in range(2):
-                        products(ob[:, 256 * jj + P * c:256 * jj + P * (c + 1)], 2 * t + jj, xqa, P * c, sq0, P * c)
-                for jj in range(2):
-                    relu("s", oa[:, 2 * t + jj, :], ob[:, 256 * jj:256 * (jj + 1)], 2 * t + jj)
-                nc.sync.dma_start(out=oview[:, 2 * t:2 * t + 2, 0:256], in_=oa[:, 2 * t:2 * t + 2, :])
-        sq1 = gather_skip(1, "hold0", "hold1")
-        xqc = finish_x("c", 1, xc_)
-        obc = keep.tile([P, 4, 256], F32, name="obc")
+        for h in range(2):
+            ob = bank(6 + h)
+            for jj in range(2):
+                for c in range(2):
+                    products(ob[:, 256 * jj + P * c:256 * jj + P * (c + 1)], 2 * h + jj, xqa, P * c, sq0, P * c)
+            for jj in range(2):
+                relu("s", oa[:, 2 * h + jj, :], ob[:, 256 * jj:256 * (jj + 1)], 2 * h + jj)
+            nc.sync.dma_start(out=oview[:, 2 * h:2 * h + 2, 0:256], in_=oa[:, 2 * h:2 * h + 2, :])
+        zc = bank(4)
+        chunk(3, 1, (0, 1), zc)
+        xqb = finish_x("b", 1, zb, "g0")
+        sq1 = gather_skip(1, "g3", "g4")
+        xqc = finish_x("c", 1, zc)
+        o2 = keep.tile([P, 4, P], F32, name="o2")
+        o3 = keep.tile([P, 4, P], F32, name="o3")
+        ob = bank(1)
         for j in range(4):
-            ob = bank(4 + j)
-            products(ob[:, 0:P], j, xqb, 0, sq1, 0)
-            products(ob[:, P:2 * P], j, xqc, 0, sq1, P)
-            relu("sv"[j % 2], obc[:, j, :], ob[:, 0:256], j)
+            products(ob[:, P * j:P * (j + 1)], j, xqb, 0, sq1, 0)
+        for j in range(4):
+            relu("s", o2[:, j, :], ob[:, P * j:P * (j + 1)], j)
+        nc.sync.dma_start(out=oview[:, :, 256:384], in_=o2[:])
+        for j in range(4):
+            ob = bank((2, 3, 6, 7)[j])
+            products(ob[:, 0:P], j, xqc, 0, sq1, P)
+            relu("vvsv"[j], o3[:, j, :], ob[:, 0:P], j)
             if j % 2 == 1:
-                nc.sync.dma_start(out=oview[:, j - 1:j + 1, 256:512], in_=obc[:, j - 1:j + 1, :])
+                nc.sync.dma_start(out=oview[:, j - 1:j + 1, 384:512], in_=o3[:, j - 1:j + 1, :])

@@ -32,7 +32,7 @@ def tile_attend_threenn_kernel(tc, coarse, wa, wb, wc, wf, skip_words, skip_scal
 
         lists = [keep.tile([P, NI // 16], U16, name="list%d" % l) for l in range(4)]
         planes = [keep.tile([P, U], F32, name="plane%d" % t) for t in range(4)]
-        wcol = [keep.tile([P, 4], F32, name="wcol%d" % l) for l in range(3)]
+        wcol = [keep.tile([P, 4], F32, name=nm, align_bytes=64) for nm in ("wcol0", "wcol1", "wcol2")]
         bcol = keep.tile([P, 4], F32, name="bcol")
         ident = keep.tile([P, P], F32, name="ident")
         sk_w = keep.tile([P, T], U16, name="sk_w")
@@ -43,12 +43,11 @@ def tile_attend_threenn_kernel(tc, coarse, wa, wb, wc, wf, skip_words, skip_scal
         scal = {}
         for n in ("wf", "ws"):
             raw[n] = [keep.tile([P, 4, F // 2], F32, name="raw_%s%d" % (n, h), align_bytes=64) for h in range(2)]
-            codes[n] = keep.tile([P, F], U32, name="codes_" + n, align_bytes=64)
             scal[n] = keep.tile([P, F], U8, name="scal_" + n, align_bytes=64)
 
         wbc = [keep.tile([P, NI], F32, name="wbc%d" % l) for l in range(3)]
         make_identity(nc, ident[:])
-        nc.vector.memset(sk_s[:].bitcast(I32), 0)
+        nc.gpsimd.memset(sk_s[:].bitcast(I32), 0)
 
         cview = coarse.rearrange("(p t) u -> p t u", t=4)
         wview = {"wf": wf.rearrange("(p t) f -> p t f", t=4), "ws": ws.rearrange("(p t) f -> p t f", t=4)}
@@ -59,19 +58,18 @@ def tile_attend_threenn_kernel(tc, coarse, wa, wb, wc, wf, skip_words, skip_scal
         def load_w(n, h):
             nc.sync.dma_start(out=raw[n][h][:], in_=wview[n][:, :, 256 * h:256 * (h + 1)])
 
-        load_col(0)
+        for l in range(3):
+            load_col(l)
         nc.sync.dma_start(lists[0][:], offs)
         nc.sync.dma_start(out=planes[0][:], in_=cview[:, 0, :])
-        load_col(1)
         nc.sync.dma_start(lists[1][:], offs2)
-        load_col(2)
         nc.sync.dma_start(lists[2][:], offs3)
         load_w("wf", 0)
-        nc.sync.dma_start(out=planes[1][:], in_=cview[:, 1, :])
         load_w("wf", 1)
-        nc.sync.dma_start(out=planes[2][:], in_=cview[:, 2, :])
+        nc.sync.dma_start(out=planes[1][:], in_=cview[:, 1, :])
         load_w("ws", 0)
         load_w("ws", 1)
+        nc.sync.dma_start(out=planes[2][:], in_=cview[:, 2, :])
         nc.sync.dma_start(out=planes[3][:], in_=cview[:, 3, :])
         nc.sync.dma_start(lists[3][:], offs4)
         nc.sync.dma_start(out=sk_w[:].bitcast(I32), in_=skip_words[0].bitcast(I32))
@@ -85,7 +83,8 @@ def tile_attend_threenn_kernel(tc, coarse, wa, wb, wc, wf, skip_words, skip_scal
             b = bank(5 + l)
             for c in range(4):
                 nc.tensor.transpose(b[:, P * c:P * (c + 1)], wcol[l][:, c:c + 1].to_broadcast([P, P]), ident[:])
-            nc.scalar.copy(out=wbc[l][:].rearrange("p (n c) -> p n c", c=4), in_=b[:].rearrange("p (c n) -> p n c", c=4))
+            cp = nc.vector.tensor_copy if l == 0 else nc.scalar.copy
+            cp(out=wbc[l][:].rearrange("p (n c) -> p n c", c=4), in_=b[:].rearrange("p (c n) -> p n c", c=4))
 
         def interleave(n, j):
             src = raw[n][j // 2][:, :, P * (j % 2):P * (j % 2 + 1)].rearrange("p t (c i) -> p c t i", i=4)
@@ -93,39 +92,40 @@ def tile_attend_threenn_kernel(tc, coarse, wa, wb, wc, wf, skip_words, skip_scal
             nc.scalar.copy(out=dst, in_=src)
 
         def quant_w(n):
+            codes[n] = keep.tile([P, F], U32, name="codes_" + n, align_bytes=64)
             nc.vector.quantize_mx(out=codes[n][:].bitcast(FP8X4), scales=scal[n][:],
                                   in_=grp[n][:].rearrange("p f t -> p (f t)"))
 
         def unit(t, l, c0, nch, ydst, tag=None):
             n = P * nch
             slot = (3 * t + l) % 6
-            g = keep.tile([P, n], F32, name=tag or "g%d" % slot, align_bytes=64)
-            nc.vector.tensor_tensor(g[:], planes[t][:].indirect(lists[l][:, 8 * c0:8 * (c0 + nch)]),
+            g = tag()
+            nc.vector.tensor_tensor(g, planes[t][:].indirect(lists[l][:, 8 * c0:8 * (c0 + nch)]),
                                     wbc[l][:, P * c0:P * (c0 + nch)], ALU.mult)
             return g
 
-        def turn(y, nch, u, z, name):
-            xb = ring.tile([P, nch, P, 2], BF16, name="xb", align_bytes=64)
-            nc.scalar.copy(out=xb[:], in_=y[:, 0:256 * nch].rearrange("i (c e p) -> i c p e", c=nch, e=2))
-            words = xb[:].rearrange("i c p e -> i (c p e)").bitcast(F32)
+        def turn(y, nch, u, z, xb):
+            nc.scalar.copy(out=xb, in_=y[:, 0:256 * nch].rearrange("i (c e p) -> i c p e", c=nch, e=2))
+            words = xb.rearrange("i c p e -> i (c p e)").bitcast(F32)
             for c in range(nch):
-                nc.tensor.transpose(z[:, 256 * c + P * u:256 * c + P * (u + 1)], words[:, P * c:P * (c + 1)], ident[:])
+                nc.tensor.transpose(z[c][:, P * u:P * (u + 1)], words[:, P * c:P * (c + 1)], ident[:])
 
-        def finish_x(name, nch, z, tag=None):
-            xg = keep.tile([P, P * nch * 4], BF16, name="xg" + name, align_bytes=64)
+        def finish_x(name, nch, z, tag=None, gtag=None):
+            xg = keep.tile([P, P * nch * 4], BF16, name=gtag or "xg" + name, align_bytes=64)
             xc = keep.tile([P, P * nch], U32, name=tag or "xc" + name, align_bytes=64)
             xs = keep.tile([P, P * nch], U8, name="xs" + name, align_bytes=64)
             nc.scalar.copy(out=xg[:].bitcast(F32).rearrange("p (c i u) -> p c i u", c=nch, u=2),
-                           in_=z[:, 0:256 * nch].rearrange("p (c u i) -> p c i u", c=nch, u=2))
+                           in_=z.rearrange("p (c u i) -> p c i u", c=nch, u=2))
             nc.vector.quantize_mx(out=xc[:].bitcast(FP8X4), scales=xs[:], in_=xg[:])
             return xc, xs
 
-        def plane(t, c0, nch, ydst, tags={}):
-            gs = [unit(t, l, c0, nch, ydst, tags.get(l)) for l in range(3)]
-            for c in range(nch):
-                for l in range(3):
-                    nc.tensor.matmul(ydst[c], gs[l][:, P * c:P * (c + 1)], ident[:],
-                                     start=(l == 0), stop=(l == 2), is_transpose=True)
+        def plane(t, c0, nch, ydst, tags):
+            order = (2, 0, 1) if t == 1 else (0, 1, 2)
+            for l in order:
+                g = unit(t, l, c0, nch, ydst, tags[l])
+                for c in range(nch):
+                    nc.tensor.matmul(ydst[c], g[:, P * c:P * (c + 1)], ident[:],
+                                     start=(l == order[0]), stop=(l == order[2]), is_transpose=True)
 
         def gather_skip(h, tag_w, tag_s):
             gw = keep.tile([P, 256], U16, name=tag_w, align_bytes=64)
@@ -152,31 +152,60 @@ def tile_attend_threenn_kernel(tc, coarse, wa, wb, wc, wf, skip_words, skip_scal
 
         oview = out.rearrange("(j p) i -> p j i", p=P)
 
-        def chunk(c0, nch, ybanks, z, tags={}, after={}):
-            for u in range(2):
-                y = bank(ybanks[u])
-                for e in range(2):
-                    t = 2 * u + e
-                    plane(t, c0, nch, [y[:, 256 * c + P * e:256 * c + P * (e + 1)] for c in range(nch)],
-                          {l: tags[(t, l)] for l in range(3) if (t, l) in tags})
-                turn(y, nch, u, z, "")
-                if u in after:
-                    after[u]()
+        def half(u, c0, nch, ybanks, z, tags={}, between=()):
+            ys = [bank(b) for b in ybanks]
+            per = nch // len(ys)
+            for e in range(2):
+                t = 2 * u + e
+                plane(t, c0, nch, [ys[c // per][:, 256 * (c % per) + P * e:256 * (c % per) + P * (e + 1)] for c in range(nch)],
+                      {l: tags[(t, l)] for l in range(3) if (t, l) in tags})
+            for step in between:
+                step()
+            xb = keep.tile([P, nch, P, 2], BF16, name="xb%d_%d" % (u, c0), align_bytes=64)
+            for k, y in enumerate(ys):
+                if z[k] is None:
+                    xw = turn_out(y, xb[:, k:k + 1])
+                    z[k] = bank(3)[:, 0:256]
+                    nc.tensor.transpose(z[k][:, P * u:P * (u + 1)], xw, ident[:])
+                else:
+                    turn(y, per, u, z[per * k:per * (k + 1)], xb[:, per * k:per * (k + 1)])
+
+        def turn_out(y, xb):
+            nc.scalar.copy(out=xb, in_=y[:, 0:256].rearrange("i (c e p) -> i c p e", c=1, e=2))
+            return xb.rearrange("i c p e -> i (c p e)").bitcast(F32)
 
         def prep(n):
             grp[n] = keep.tile([P, F, 4], BF16, name="grp_" + n, align_bytes=64)
             for j in range(4):
                 interleave(n, j)
-            quant_w(n)
+
+        held = {}
+
+        def lend(name, key, n, k=0, of=1):
+            def get():
+                if key not in held:
+                    held[key] = keep.tile([P, of, n], F32, name=name, align_bytes=64)
+                return held[key][:, k, :]
+            return get
 
         za = bank(4)
-        chunk(0, 2, (0, 1), za, {(0, 2): "grp_wf"})
-        prep("wf")
-        prep("ws")
-        sq0 = gather_skip(0, "gw0", "gs0")
-        xqa = finish_x("a", 2, za)
         zb = bank(5)
-        chunk(2, 1, (2, 3), zb)
+        zs = [za[:, 0:256], za[:, 256:512], zb[:, 0:256], None]
+        half(0, 0, 4, (0, 1, 2, 3), zs,
+             {(0, 0): lend("grp_wf", 0, NI), (0, 1): lend("grp_ws", 1, NI), (0, 2): lend("s0", 2, NI),
+              (1, 2): lend("s1", 3, NI), (1, 0): lend("s0", 4, NI), (1, 1): lend("s1", 5, NI)},
+             (lambda: prep("wf"), lambda: prep("ws")))
+        quant_w("wf")
+        quant_w("ws")
+        half(1, 0, 2, (6, 7), zs[0:2],
+             {(2, 0): lend("s0", 6, 256, 0, 2), (2, 1): lend("s0", 6, 256, 1, 2), (2, 2): lend("s1", 7, 256, 0, 2),
+              (3, 0): lend("s1", 7, 256, 1, 2), (3, 1): lend("s0", 8, 256, 0, 2), (3, 2): lend("s0", 8, 256, 1, 2)})
+        xqa = finish_x("a", 2, za[:])
+        half(1, 2, 1, (0,), zs[2:3],
+             {(2, 0): lend("s1", 9, P, 0, 2), (2, 1): lend("s1", 9, P, 1, 2), (2, 2): lend("s0", 10, P),
+              (3, 0): lend("xb1_0", 11, P, 0, 3), (3, 1): lend("xb1_0", 11, P, 1, 3), (3, 2): lend("xb1_0", 11, P, 2, 3)})
+        sq0 = gather_skip(0, "s1", "s0")
+        xqb = finish_x("b", 1, zs[2])
         oa = keep.tile([P, 4, 256], F32, name="oa")
         for h in range(2):
             ob = bank(6 + h)
@@ -186,11 +215,9 @@ def tile_attend_threenn_kernel(tc, coarse, wa, wb, wc, wf, skip_words, skip_scal
             for jj in range(2):
                 relu("s", oa[:, 2 * h + jj, :], ob[:, 256 * jj:256 * (jj + 1)], 2 * h + jj)
             nc.sync.dma_start(out=oview[:, 2 * h:2 * h + 2, 0:256], in_=oa[:, 2 * h:2 * h + 2, :])
-        zc = bank(4)
-        chunk(3, 1, (0, 1), zc)
-        xqb = finish_x("b", 1, zb, "g0")
-        sq1 = gather_skip(1, "g3", "g4")
-        xqc = finish_x("c", 1, zc)
+        half(1, 3, 1, (1,), zs[3:4], {(t, l): lend("xga", 12, P, 3 * (t - 2) + l, 6) for t in (2, 3) for l in range(3)})
+        sq1 = gather_skip(1, "xgb", "xga")
+        xqc = finish_x("c", 1, zs[3])
         o2 = keep.tile([P, 4, P], F32, name="o2")
         o3 = keep.tile([P, 4, P], F32, name="o3")
         ob = bank(1)
@@ -200,7 +227,7 @@ def tile_attend_threenn_kernel(tc, coarse, wa, wb, wc, wf, skip_words, skip_scal
             relu("s", o2[:, j, :], ob[:, P * j:P * (j + 1)], j)
         nc.sync.dma_start(out=oview[:, :, 256:384], in_=o2[:])
         for j in range(4):
-            ob = bank((2, 3, 6, 7)[j])
+            ob = bank((0, 2, 6, 7)[j])
             products(ob[:, 0:P], j, xqc, 0, sq1, P)
             relu("vvsv"[j], o3[:, j, :], ob[:, 0:P], j)
             if j % 2 == 1:

@@ -152,7 +152,7 @@ def tile_attend_threenn_kernel(tc, coarse, wa, wb, wc, wf, skip_words, skip_scal
 
         oview = out.rearrange("(j p) i -> p j i", p=P)
 
-        def half(u, c0, nch, ybanks, z, tags={}, between=()):
+        def half(u, c0, nch, ybanks, z, tags={}, between=(), xb=None):
             ys = [bank(b) for b in ybanks]
             per = nch // len(ys)
             for e in range(2):
@@ -161,7 +161,8 @@ def tile_attend_threenn_kernel(tc, coarse, wa, wb, wc, wf, skip_words, skip_scal
                       {l: tags[(t, l)] for l in range(3) if (t, l) in tags})
             for step in between:
                 step()
-            xb = keep.tile([P, nch, P, 2], BF16, name="xb%d_%d" % (u, c0), align_bytes=64)
+            if xb is None:
+                xb = keep.tile([P, nch, P, 2], BF16, name="xb%d_%d" % (u, c0), align_bytes=64)
             for k, y in enumerate(ys):
                 if z[k] is None:
                     xw = turn_out(y, xb[:, k:k + 1])
@@ -201,9 +202,11 @@ def tile_attend_threenn_kernel(tc, coarse, wa, wb, wc, wf, skip_words, skip_scal
              {(2, 0): lend("s0", 6, 256, 0, 2), (2, 1): lend("s0", 6, 256, 1, 2), (2, 2): lend("s1", 7, 256, 0, 2),
               (3, 0): lend("s1", 7, 256, 1, 2), (3, 1): lend("s0", 8, 256, 0, 2), (3, 2): lend("s0", 8, 256, 1, 2)})
         xqa = finish_x("a", 2, za[:])
+        late = keep.tile([P, 7 * P], F32, name="xga", align_bytes=64)
         half(1, 2, 1, (0,), zs[2:3],
              {(2, 0): lend("s1", 9, P, 0, 2), (2, 1): lend("s1", 9, P, 1, 2), (2, 2): lend("s0", 10, P),
-              (3, 0): lend("xb1_0", 11, P, 0, 3), (3, 1): lend("xb1_0", 11, P, 1, 3), (3, 2): lend("xb1_0", 11, P, 2, 3)})
+              (3, 0): lend("xb1_0", 11, P, 0, 3), (3, 1): lend("xb1_0", 11, P, 1, 3), (3, 2): lend("xb1_0", 11, P, 2, 3)},
+             xb=late[:, 6 * P:7 * P].bitcast(BF16).rearrange("i (c p e) -> i c p e", c=1, e=2))
         sq0 = gather_skip(0, "s1", "s0")
         xqb = finish_x("b", 1, zs[2])
         oa = keep.tile([P, 4, 256], F32, name="oa")
@@ -215,7 +218,10 @@ def tile_attend_threenn_kernel(tc, coarse, wa, wb, wc, wf, skip_words, skip_scal
             for jj in range(2):
                 relu("s", oa[:, 2 * h + jj, :], ob[:, 256 * jj:256 * (jj + 1)], 2 * h + jj)
             nc.sync.dma_start(out=oview[:, 2 * h:2 * h + 2, 0:256], in_=oa[:, 2 * h:2 * h + 2, :])
-        half(1, 3, 1, (1,), zs[3:4], {(t, l): lend("xga", 12, P, 3 * (t - 2) + l, 6) for t in (2, 3) for l in range(3)})
+        def piece(k):
+            return lambda: late[:, P * k:P * (k + 1)]
+
+        half(1, 3, 1, (1,), zs[3:4], {(t, l): piece(3 * (t - 2) + l) for t in (2, 3) for l in range(3)})
         sq1 = gather_skip(1, "xgb", "xga")
         xqc = finish_x("c", 1, zs[3])
         o2 = keep.tile([P, 4, P], F32, name="o2")

@@ -20,128 +20,149 @@ FLOPS = 2 * (K + R) * NI * F
 
 
 def tile_attend_threenn_kernel(tc, coarse, wa, wb, wc, wf, skip_words, skip_scales, ws, bias,
-                                offs, offs2, offs3, offs4, out):
+                                    offs, offs2, offs3, offs4, out):
     nc = tc.nc
     with ExitStack() as ctx:
         keep = ctx.enter_context(tc.tile_pool(name="keep", bufs=1))
-        ring = ctx.enter_context(tc.tile_pool(name="ring", bufs=6))
         psum = ctx.enter_context(tc.psum_pool(name="psum", bufs=1))
+        made = []
+
+        def sb(shape, dtype, tag):
+            made.append(tag)
+            return keep.tile(shape, dtype, name="%s_%d" % (tag, len(made)), tag=tag, align_bytes=64)
 
         def bank(b):
-            return psum.tile([P, 512], F32, name="bank%d" % b)
+            made.append(b)
+            return psum.tile([P, 512], F32, name="bank%d_%d" % (b, len(made)), tag="bank%d" % b)
 
-        lists = [keep.tile([P, NI // 16], U16, name="list%d" % l) for l in range(4)]
-        planes = [keep.tile([P, U], F32, name="plane%d" % t) for t in range(4)]
-        wcol = [keep.tile([P, 4], F32, name=nm, align_bytes=64) for nm in ("wcol0", "wcol1", "wcol2")]
-        bcol = keep.tile([P, 4], F32, name="bcol")
-        ident = keep.tile([P, P], F32, name="ident")
-        sk_w = keep.tile([P, T], U16, name="sk_w")
-        sk_s = keep.tile([P, T], U8, name="sk_s")
-        raw = {}
-        grp = {}
+        lists = [sb([P, NI // 16], U16, "list%d" % l) for l in range(4)]
+        planes = [sb([P, U], F32, "plane%d" % t) for t in range(4)]
+        wcol = [sb([P, 4], F32, "wcol%d" % l) for l in range(3)]
+        bcol = sb([P, 4], F32, "bcol")
+        ident = sb([P, P], F32, "ident")
+        sk_w = sb([P, T], U16, "sk_w")
+        sk_s = sb([P, T], U8, "sk_s")
+        raw = {n: [sb([P, 4, F // 2], F32, "raw_%s%d" % (n, h)) for h in range(2)] for n in ("wf", "ws")}
+        scal = {n: sb([P, F], U8, "scal_" + n) for n in ("wf", "ws")}
+        grp = {n: sb([P, F, 4], BF16, "grp_" + n) for n in ("wf", "ws")}
         codes = {}
-        scal = {}
-        for n in ("wf", "ws"):
-            raw[n] = [keep.tile([P, 4, F // 2], F32, name="raw_%s%d" % (n, h), align_bytes=64) for h in range(2)]
-            scal[n] = keep.tile([P, F], U8, name="scal_" + n, align_bytes=64)
+        wrow = [sb([P, NI], F32, "wrow%d" % l) for l in range(2)]
 
-        wbc = [keep.tile([P, NI], F32, name="wbc%d" % l) for l in range(3)]
         make_identity(nc, ident[:])
         nc.gpsimd.memset(sk_s[:].bitcast(I32), 0)
 
         cview = coarse.rearrange("(p t) u -> p t u", t=4)
         wview = {"wf": wf.rearrange("(p t) f -> p t f", t=4), "ws": ws.rearrange("(p t) f -> p t f", t=4)}
 
-        def load_col(l):
-            nc.sync.dma_start(out=wcol[l][:], in_=(wa, wb, wc)[l].rearrange("o (p c) -> p (o c)", c=4))
-
         def load_w(n, h):
             nc.sync.dma_start(out=raw[n][h][:], in_=wview[n][:, :, 256 * h:256 * (h + 1)])
 
         for l in range(3):
-            load_col(l)
+            nc.sync.dma_start(out=wcol[l][:], in_=(wa, wb, wc)[l].rearrange("o (p c) -> p (o c)", c=4))
         nc.sync.dma_start(lists[0][:], offs)
+        nc.sync.dma_start(lists[2][:], offs3)
         nc.sync.dma_start(out=planes[0][:], in_=cview[:, 0, :])
         nc.sync.dma_start(lists[1][:], offs2)
-        nc.sync.dma_start(lists[2][:], offs3)
+        for t in range(1, 4):
+            nc.sync.dma_start(out=planes[t][:], in_=cview[:, t, :])
         load_w("wf", 0)
         load_w("wf", 1)
-        nc.sync.dma_start(out=planes[1][:], in_=cview[:, 1, :])
-        load_w("ws", 0)
-        load_w("ws", 1)
-        nc.sync.dma_start(out=planes[2][:], in_=cview[:, 2, :])
-        nc.sync.dma_start(out=planes[3][:], in_=cview[:, 3, :])
         nc.sync.dma_start(lists[3][:], offs4)
-        nc.sync.dma_start(out=sk_w[:].bitcast(I32), in_=skip_words[0].bitcast(I32))
         for q in range(4):
             nc.sync.dma_start(out=sk_s[:].bitcast(I32)[32 * q:32 * q + 4, :],
                               in_=skip_scales[0].bitcast(I32)[4 * q:4 * q + 4, :])
+        nc.sync.dma_start(out=sk_w[:].bitcast(I32), in_=skip_words[0].bitcast(I32))
+        load_w("ws", 0)
+        load_w("ws", 1)
         with nc.allow_non_contiguous_dma(reason="one bias value a partition"):
             nc.sync.dma_start(out=bcol[:], in_=bias.rearrange("(j p) o -> p (j o)", p=P))
 
+        wbank = []
         for l in range(3):
-            b = bank(5 + l)
+            b = bank((4, 5, 7)[l])
             for c in range(4):
                 nc.tensor.transpose(b[:, P * c:P * (c + 1)], wcol[l][:, c:c + 1].to_broadcast([P, P]), ident[:])
-            cp = nc.vector.tensor_copy if l == 0 else nc.scalar.copy
-            cp(out=wbc[l][:].rearrange("p (n c) -> p n c", c=4), in_=b[:].rearrange("p (c n) -> p n c", c=4))
+            wbank.append(b[:].rearrange("p (c n) -> p n c", c=4))
+        nc.scalar.copy(out=wrow[0][:].rearrange("p (n c) -> p n c", c=4), in_=wbank[0])
+        nc.scalar.copy(out=wrow[1][:].rearrange("p (n c) -> p n c", c=4), in_=wbank[1])
 
-        def interleave(n, j):
-            src = raw[n][j // 2][:, :, P * (j % 2):P * (j % 2 + 1)].rearrange("p t (c i) -> p c t i", i=4)
-            dst = grp[n][:, P * j:P * (j + 1), :].rearrange("p (c i) t -> p c t i", i=4)
-            nc.scalar.copy(out=dst, in_=src)
+        last = sb([P, 3 * NI], F32, "wcol2")
+        plain = {(0, 2): sb([P, NI], F32, "wcol0")[:], (1, 2): sb([P, NI], F32, "wcol1")[:],
+                 (2, 2): last[:, 0:NI], (3, 1): last[:, NI:2 * NI], (3, 2): last[:, 2 * NI:3 * NI]}
+        for (t, l), dst in plain.items():
+            nc.scalar.activation(out=dst, in_=planes[t][:].indirect(lists[l][:]), func=ACT.Copy)
 
-        def quant_w(n):
-            codes[n] = keep.tile([P, F], U32, name="codes_" + n, align_bytes=64)
+        def interleave(n, h):
+            for j in (2 * h, 2 * h + 1):
+                src = raw[n][h][:, :, P * (j % 2):P * (j % 2 + 1)].rearrange("p t (c i) -> p c t i", i=4)
+                dst = grp[n][:, P * j:P * (j + 1), :].rearrange("p (c i) t -> p c t i", i=4)
+                nc.scalar.copy(out=dst, in_=src)
+
+        def quant_w(n, tag):
+            codes[n] = sb([P, F], U32, tag)
             nc.vector.quantize_mx(out=codes[n][:].bitcast(FP8X4), scales=scal[n][:],
                                   in_=grp[n][:].rearrange("p f t -> p (f t)"))
 
-        def unit(t, l, c0, nch, ydst, tag=None):
+        def weighted(u, c0, nch, ys, dsts, es=(0, 1)):
             n = P * nch
-            slot = (3 * t + l) % 6
-            g = tag()
-            nc.vector.tensor_tensor(g, planes[t][:].indirect(lists[l][:, 8 * c0:8 * (c0 + nch)]),
-                                    wbc[l][:, P * c0:P * (c0 + nch)], ALU.mult)
-            return g
+            per = min(nch, 2)
+            for e in es:
+                t = 2 * u + e
+                for l in range(3):
+                    g = dsts[3 * e + l]()
+                    if (t, l) not in plain:
+                        nc.vector.tensor_tensor(g, planes[t][:].indirect(lists[l][:, 8 * c0:8 * (c0 + nch)]),
+                                                wrow[l][:, P * c0:P * c0 + n], ALU.mult)
+                    elif l < 2:
+                        nc.vector.tensor_tensor(g, plain[(t, l)][:, P * c0:P * c0 + n], wrow[l][:, P * c0:P * c0 + n], ALU.mult)
+                    else:
+                        nc.vector.tensor_tensor(g.rearrange("p (n c) -> p n c", c=4),
+                                                plain[(t, l)][:, P * c0:P * c0 + n].rearrange("p (n c) -> p n c", c=4),
+                                                wbank[2][:, 32 * c0:32 * (c0 + nch), :], ALU.mult)
+                    for c in range(nch):
+                        col = 256 * (c % 2) + P * e
+                        nc.tensor.matmul(ys[c // 2][:, col:col + P], g[:, P * c:P * (c + 1)], ident[:],
+                                         start=(e == 0 and l == 0 and c % 2 == 0),
+                                         stop=(e == 1 and l == 2 and c % 2 == per - 1), is_transpose=True)
 
-        def turn(y, nch, u, z, xb):
+        def ring(n, tags):
+            return [lambda tag=tag: sb([P, n], F32, tag)[:] for tag in tags]
+
+        def parts(tag, k, n):
+            whole = sb([P, k * n], F32, tag)
+            return [lambda i=i: whole[:, n * i:n * (i + 1)] for i in range(k)]
+
+        def turn(y, nch, u, zs, words):
+            xb = words.bitcast(BF16).rearrange("i (c p e) -> i c p e", c=nch, e=2)
             nc.scalar.copy(out=xb, in_=y[:, 0:256 * nch].rearrange("i (c e p) -> i c p e", c=nch, e=2))
-            words = xb.rearrange("i c p e -> i (c p e)").bitcast(F32)
-            for c in range(nch):
-                nc.tensor.transpose(z[c][:, P * u:P * (u + 1)], words[:, P * c:P * (c + 1)], ident[:])
+            return lambda: back(nch, u, zs, words)
 
-        def finish_x(name, nch, z, tag=None, gtag=None):
-            xg = keep.tile([P, P * nch * 4], BF16, name=gtag or "xg" + name, align_bytes=64)
-            xc = keep.tile([P, P * nch], U32, name=tag or "xc" + name, align_bytes=64)
-            xs = keep.tile([P, P * nch], U8, name="xs" + name, align_bytes=64)
-            nc.scalar.copy(out=xg[:].bitcast(F32).rearrange("p (c i u) -> p c i u", c=nch, u=2),
+        def back(nch, u, zs, words):
+            for c in range(nch):
+                nc.tensor.transpose(zs[c][:, P * u:P * (u + 1)], words[:, P * c:P * (c + 1)], ident[:])
+
+        def weave(nch, z, words):
+            xg = words.bitcast(BF16)
+            nc.scalar.copy(out=words.rearrange("p (c i u) -> p c i u", c=nch, u=2),
                            in_=z.rearrange("p (c u i) -> p c i u", c=nch, u=2))
-            nc.vector.quantize_mx(out=xc[:].bitcast(FP8X4), scales=xs[:], in_=xg[:])
+            return xg
+
+        def quant_x(name, nch, xg):
+            xc = sb([P, P * nch], U32, "xc" + name)
+            xs = sb([P, P * nch], U8, "xs" + name)
+            nc.vector.quantize_mx(out=xc[:].bitcast(FP8X4), scales=xs[:], in_=xg)
             return xc, xs
 
-        def plane(t, c0, nch, ydst, tags):
-            order = (2, 0, 1) if t == 1 else (0, 1, 2)
-            for l in order:
-                g = unit(t, l, c0, nch, ydst, tags[l])
-                for c in range(nch):
-                    nc.tensor.matmul(ydst[c], g[:, P * c:P * (c + 1)], ident[:],
-                                     start=(l == order[0]), stop=(l == order[2]), is_transpose=True)
+        def gather_skip(table, h, dtype, tag):
+            g = sb([P, 256], dtype, tag)
+            nc.vector.tensor_copy(g[:], table[:].indirect(lists[3][:, 16 * h:16 * (h + 1)]))
+            return g
 
-        def gather_skip(h, tag_w, tag_s):
-            gw = keep.tile([P, 256], U16, name=tag_w, align_bytes=64)
-            gs = keep.tile([P, 256], U8, name=tag_s, align_bytes=64)
-            nc.vector.tensor_copy(gw[:], sk_w[:].indirect(lists[3][:, 16 * h:16 * (h + 1)]))
-            nc.vector.tensor_copy(gs[:], sk_s[:].indirect(lists[3][:, 16 * h:16 * (h + 1)]))
-            return gw, gs
-
-        def products(dst, j, xq, xo, sq, so):
+        def product(dst, n, j, q, o, width, start, stop):
             fc = slice(P * j, P * (j + 1))
-            nc.tensor.matmul_mx(out=dst, lhsT=codes["wf"][:, fc].bitcast(FP8X4), lhsT_scale=scal["wf"][:, fc],
-                                rhs=xq[0][:, xo:xo + P].bitcast(FP8X4), rhs_scale=xq[1][:, xo:xo + P],
-                                start=True, stop=False)
-            nc.tensor.matmul_mx(out=dst, lhsT=codes["ws"][:, fc].bitcast(FP8X4), lhsT_scale=scal["ws"][:, fc],
-                                rhs=sq[0][:, so:so + P].bitcast(FP4X4), rhs_scale=sq[1][:, so:so + P],
-                                start=False, stop=True)
+            nc.tensor.matmul_mx(out=dst, lhsT=codes[n][:, fc].bitcast(FP8X4), lhsT_scale=scal[n][:, fc],
+                                rhs=q[0][:, o:o + width].bitcast(FP8X4 if n == "wf" else FP4X4),
+                                rhs_scale=q[1][:, o:o + width], start=start, stop=stop)
 
         def relu(eng, dst, src, j):
             bj = bcol[:, j:j + 1]
@@ -152,89 +173,52 @@ def tile_attend_threenn_kernel(tc, coarse, wa, wb, wc, wf, skip_words, skip_scal
 
         oview = out.rearrange("(j p) i -> p j i", p=P)
 
-        def half(u, c0, nch, ybanks, z, tags={}, between=(), xb=None):
-            ys = [bank(b) for b in ybanks]
-            per = nch // len(ys)
-            for e in range(2):
-                t = 2 * u + e
-                plane(t, c0, nch, [ys[c // per][:, 256 * (c % per) + P * e:256 * (c % per) + P * (e + 1)] for c in range(nch)],
-                      {l: tags[(t, l)] for l in range(3) if (t, l) in tags})
-            for step in between:
-                step()
-            if xb is None:
-                xb = keep.tile([P, nch, P, 2], BF16, name="xb%d_%d" % (u, c0), align_bytes=64)
-            for k, y in enumerate(ys):
-                if z[k] is None:
-                    xw = turn_out(y, xb[:, k:k + 1])
-                    z[k] = bank(3)[:, 0:256]
-                    nc.tensor.transpose(z[k][:, P * u:P * (u + 1)], xw, ident[:])
-                else:
-                    turn(y, per, u, z[per * k:per * (k + 1)], xb[:, per * k:per * (k + 1)])
-
-        def turn_out(y, xb):
-            nc.scalar.copy(out=xb, in_=y[:, 0:256].rearrange("i (c e p) -> i c p e", c=1, e=2))
-            return xb.rearrange("i c p e -> i (c p e)").bitcast(F32)
-
-        def prep(n):
-            grp[n] = keep.tile([P, F, 4], BF16, name="grp_" + n, align_bytes=64)
-            for j in range(4):
-                interleave(n, j)
-
-        held = {}
-
-        def lend(name, key, n, k=0, of=1):
-            def get():
-                if key not in held:
-                    held[key] = keep.tile([P, of, n], F32, name=name, align_bytes=64)
-                return held[key][:, k, :]
-            return get
-
+        y0 = [bank(0), bank(1)]
+        weighted(0, 0, 4, y0, ring(NI, ("r0", "r1", "r2", "r0", "r1", "r2")))
+        interleave("wf", 0)
+        interleave("wf", 1)
         za = bank(4)
         zb = bank(5)
-        zs = [za[:, 0:256], za[:, 256:512], zb[:, 0:256], None]
-        half(0, 0, 4, (0, 1, 2, 3), zs,
-             {(0, 0): lend("grp_wf", 0, NI), (0, 1): lend("grp_ws", 1, NI), (0, 2): lend("s0", 2, NI),
-              (1, 2): lend("s1", 3, NI), (1, 0): lend("s0", 4, NI), (1, 1): lend("s1", 5, NI)},
-             (lambda: prep("wf"), lambda: prep("ws")))
-        quant_w("wf")
-        quant_w("ws")
-        half(1, 0, 2, (6, 7), zs[0:2],
-             {(2, 0): lend("s0", 6, 256, 0, 2), (2, 1): lend("s0", 6, 256, 1, 2), (2, 2): lend("s1", 7, 256, 0, 2),
-              (3, 0): lend("s1", 7, 256, 1, 2), (3, 1): lend("s0", 8, 256, 0, 2), (3, 2): lend("s0", 8, 256, 1, 2)})
-        xqa = finish_x("a", 2, za[:])
-        late = keep.tile([P, 7 * P], F32, name="xga", align_bytes=64)
-        half(1, 2, 1, (0,), zs[2:3],
-             {(2, 0): lend("s1", 9, P, 0, 2), (2, 1): lend("s1", 9, P, 1, 2), (2, 2): lend("s0", 10, P),
-              (3, 0): lend("xb1_0", 11, P, 0, 3), (3, 1): lend("xb1_0", 11, P, 1, 3), (3, 2): lend("xb1_0", 11, P, 2, 3)},
-             xb=late[:, 6 * P:7 * P].bitcast(BF16).rearrange("i (c p e) -> i c p e", c=1, e=2))
-        sq0 = gather_skip(0, "s1", "s0")
-        xqb = finish_x("b", 1, zs[2])
-        oa = keep.tile([P, 4, 256], F32, name="oa")
-        for h in range(2):
-            ob = bank(6 + h)
-            for jj in range(2):
-                for c in range(2):
-                    products(ob[:, 256 * jj + P * c:256 * jj + P * (c + 1)], 2 * h + jj, xqa, P * c, sq0, P * c)
-            for jj in range(2):
-                relu("s", oa[:, 2 * h + jj, :], ob[:, 256 * jj:256 * (jj + 1)], 2 * h + jj)
-            nc.sync.dma_start(out=oview[:, 2 * h:2 * h + 2, 0:256], in_=oa[:, 2 * h:2 * h + 2, :])
-        def piece(k):
-            return lambda: late[:, P * k:P * (k + 1)]
+        zs = [za[:, 0:256], za[:, 256:512], zb[:, 0:256], zb[:, 256:512]]
+        ya = bank(2)
+        weighted(1, 0, 2, [ya], ring(256, ("r0", "r1", "r2", "r0", "r1", "r2")))
+        quant_w("wf", "r0")
+        mid = sb([P, 4 * P], F32, "raw_wf1")
+        turn(y0[0], 2, 0, zs[0:2], mid[:, 0:2 * P])()
+        turn(ya, 2, 1, zs[0:2], mid[:, 2 * P:4 * P])()
+        interleave("ws", 0)
+        xga = weave(2, za[:], sb([P, 4 * P], F32, "xga")[:])
+        turn(y0[1], 2, 0, zs[2:4], sb([P, 2 * P], F32, "raw_ws0")[:])()
+        yb = bank(3)
+        four = parts("grp_wf", 4, 256)
+        weighted(1, 2, 2, [yb], four[0:3] + ring(256, ("r1", "r2")) + four[3:4], (0,))
+        xq = [quant_x("a", 2, xga)]
+        weighted(1, 2, 2, [yb], four[0:3] + ring(256, ("r1", "r2")) + four[3:4], (1,))
+        obs = [[bank(6), bank(0)], [bank(2), bank(1)]]
 
-        half(1, 3, 1, (1,), zs[3:4], {(t, l): piece(3 * (t - 2) + l) for t in (2, 3) for l in range(3)})
-        sq1 = gather_skip(1, "xgb", "xga")
-        xqc = finish_x("c", 1, zs[3])
-        o2 = keep.tile([P, 4, P], F32, name="o2")
-        o3 = keep.tile([P, 4, P], F32, name="o3")
-        ob = bank(1)
-        for j in range(4):
-            products(ob[:, P * j:P * (j + 1)], j, xqb, 0, sq1, 0)
-        for j in range(4):
-            relu("s", o2[:, j, :], ob[:, P * j:P * (j + 1)], j)
-        nc.sync.dma_start(out=oview[:, :, 256:384], in_=o2[:])
-        for j in range(4):
-            ob = bank((0, 2, 6, 7)[j])
-            products(ob[:, 0:P], j, xqc, 0, sq1, P)
-            relu("vvsv"[j], o3[:, j, :], ob[:, 0:P], j)
-            if j % 2 == 1:
-                nc.sync.dma_start(out=oview[:, j - 1:j + 1, 384:512], in_=o3[:, j - 1:j + 1, :])
+        def products(n, h, q):
+            for j in range(4):
+                product(obs[h][j // 2][:, 256 * (j % 2):256 * (j % 2 + 1)], n, j, q, 0, 256,
+                        n == "wf" and j % 2 == 0, n == "ws" and j % 2 == 1)
+
+        def finish(h, engines):
+            o = sb([P, 4, 256], F32, "o%d" % h)
+            for j in range(4):
+                relu(engines[j], o[:, j, :], obs[h][j // 2][:, 256 * (j % 2):256 * (j % 2 + 1)], j)
+                if j % 2 == 1:
+                    nc.sync.dma_start(out=oview[:, j - 1:j + 1, 256 * h:256 * (h + 1)], in_=o[:, j - 1:j + 1, :])
+
+        products("wf", 0, xq[0])
+        sq0 = (gather_skip(sk_w, 0, U16, "r1"), gather_skip(sk_s, 0, U8, "r2"))
+        interleave("ws", 1)
+        turn(yb, 2, 1, zs[2:4], sb([P, 2 * P], F32, "raw_ws1")[:])()
+        xgb = weave(2, zb[:], sb([P, 4 * P], F32, "xgb")[:])
+        quant_w("ws", "grp_wf")
+        products("ws", 0, sq0)
+        w1 = gather_skip(sk_w, 1, U16, "grp_ws")
+        xq.append(quant_x("b", 2, xgb))
+        products("wf", 1, xq[1])
+        sq1 = (w1, gather_skip(sk_s, 1, U8, "xgb"))
+        finish(0, "ssss")
+        products("ws", 1, sq1)
+        finish(1, "vvss")

@@ -46,10 +46,12 @@ def tile_attend_threenn_kernel(tc, coarse, wa, wb, wc, wf, skip_words, skip_scal
         scal = {n: sb([P, F], U8, "scal_" + n) for n in ("wf", "ws")}
         grp = {n: sb([P, F, 4], BF16, "grp_" + n) for n in ("wf", "ws")}
         codes = {}
-        wrow = [sb([P, NI], F32, "wrow%d" % l) for l in range(2)]
+        wrow = sb([P, NI], F32, "wrow")
 
         make_identity(nc, ident[:])
-        nc.gpsimd.memset(sk_s[:].bitcast(I32), 0)
+        sk_plane = sb([P, NI], U8, "sk_plane")
+        nc.vector.memset(sk_s[:].bitcast(I32)[0:112, :], 0)
+        nc.gpsimd.memset(sk_plane[:].bitcast(I32), 0)
 
         cview = coarse.rearrange("(p t) u -> p t u", t=4)
         wview = {"wf": wf.rearrange("(p t) f -> p t f", t=4), "ws": ws.rearrange("(p t) f -> p t f", t=4)}
@@ -57,25 +59,33 @@ def tile_attend_threenn_kernel(tc, coarse, wa, wb, wc, wf, skip_words, skip_scal
         def load_w(n, h):
             nc.sync.dma_start(out=raw[n][h][:], in_=wview[n][:, :, 256 * h:256 * (h + 1)])
 
-        for l in range(3):
+        def load_col(l):
             nc.sync.dma_start(out=wcol[l][:], in_=(wa, wb, wc)[l].rearrange("o (p c) -> p (o c)", c=4))
+
+        load_col(0)
+        nc.sync.dma_start(out=sk_s[:].bitcast(I32)[112:128, :], in_=skip_scales[0].bitcast(I32))
+        nc.sync.dma_start(lists[3][:], offs4)
+        load_col(1)
         nc.sync.dma_start(lists[0][:], offs)
         nc.sync.dma_start(lists[2][:], offs3)
+        load_col(2)
         nc.sync.dma_start(out=planes[0][:], in_=cview[:, 0, :])
         nc.sync.dma_start(lists[1][:], offs2)
         for t in range(1, 4):
             nc.sync.dma_start(out=planes[t][:], in_=cview[:, t, :])
-        load_w("wf", 0)
-        load_w("wf", 1)
-        nc.sync.dma_start(lists[3][:], offs4)
-        for q in range(4):
-            nc.sync.dma_start(out=sk_s[:].bitcast(I32)[32 * q:32 * q + 4, :],
-                              in_=skip_scales[0].bitcast(I32)[4 * q:4 * q + 4, :])
-        nc.sync.dma_start(out=sk_w[:].bitcast(I32), in_=skip_words[0].bitcast(I32))
         load_w("ws", 0)
         load_w("ws", 1)
+        nc.sync.dma_start(out=sk_w[:].bitcast(I32), in_=skip_words[0].bitcast(I32))
+        load_w("wf", 0)
+        load_w("wf", 1)
         with nc.allow_non_contiguous_dma(reason="one bias value a partition"):
             nc.sync.dma_start(out=bcol[:], in_=bias.rearrange("(j p) o -> p (j o)", p=P))
+
+        picked = sb([P, NI], U8, "picked")
+        nc.vector.tensor_copy(picked[:], sk_s[:].indirect(lists[3][:]))
+        for q in range(4):
+            nc.sync.dma_start(out=sk_plane[:].bitcast(I32)[32 * q:32 * q + 4, :],
+                              in_=picked[:].bitcast(I32)[112 + 4 * q:116 + 4 * q, :])
 
         wbank = []
         for l in range(3):
@@ -83,59 +93,48 @@ def tile_attend_threenn_kernel(tc, coarse, wa, wb, wc, wf, skip_words, skip_scal
             for c in range(4):
                 nc.tensor.transpose(b[:, P * c:P * (c + 1)], wcol[l][:, c:c + 1].to_broadcast([P, P]), ident[:])
             wbank.append(b[:].rearrange("p (c n) -> p n c", c=4))
-        nc.scalar.copy(out=wrow[0][:].rearrange("p (n c) -> p n c", c=4), in_=wbank[0])
-        nc.scalar.copy(out=wrow[1][:].rearrange("p (n c) -> p n c", c=4), in_=wbank[1])
+        nc.scalar.copy(out=wrow[:].rearrange("p (n c) -> p n c", c=4), in_=wbank[0])
 
-        last = sb([P, 3 * NI], F32, "wcol2")
-        plain = {(0, 2): sb([P, NI], F32, "wcol0")[:], (1, 2): sb([P, NI], F32, "wcol1")[:],
-                 (2, 2): last[:, 0:NI], (3, 1): last[:, NI:2 * NI], (3, 2): last[:, 2 * NI:3 * NI]}
-        for (t, l), dst in plain.items():
-            nc.scalar.activation(out=dst, in_=planes[t][:].indirect(lists[l][:]), func=ACT.Copy)
+        plain = {}
 
-        def interleave(n, h):
-            for j in (2 * h, 2 * h + 1):
-                src = raw[n][h][:, :, P * (j % 2):P * (j % 2 + 1)].rearrange("p t (c i) -> p c t i", i=4)
-                dst = grp[n][:, P * j:P * (j + 1), :].rearrange("p (c i) t -> p c t i", i=4)
-                nc.scalar.copy(out=dst, in_=src)
+        def gather_plain(u, l, c0, nch, tag):
+            plain[(u, l, c0)] = g = sb([P, 2, P * nch], F32, tag)
+            for e in range(2):
+                nc.scalar.activation(out=g[:, e, :], in_=planes[2 * u + e][:].indirect(lists[l][:, 8 * c0:8 * (c0 + nch)]),
+                                     func=ACT.Copy)
+
+        def interleave(n):
+            for j in range(4):
+                src = raw[n][j // 2][:, :, P * (j % 2):P * (j % 2 + 1)].rearrange("p t f -> p f t")
+                nc.gpsimd.tensor_scalar(out=grp[n][:, P * j:P * (j + 1), :], in0=src, scalar1=1.0, scalar2=0.0,
+                                        op0=ALU.mult, op1=ALU.add)
 
         def quant_w(n, tag):
             codes[n] = sb([P, F], U32, tag)
             nc.vector.quantize_mx(out=codes[n][:].bitcast(FP8X4), scales=scal[n][:],
                                   in_=grp[n][:].rearrange("p f t -> p (f t)"))
 
-        def weighted(u, c0, nch, ys, dsts, es=(0, 1)):
+        def add_up(g, e, nch, ys, first, last):
+            for c in range(nch):
+                col = 256 * (c % 2) + P * e
+                nc.tensor.matmul(ys[c // 2][:, col:col + P], g[:, P * c:P * (c + 1)], ident[:],
+                                 start=first and c % 2 == 0, stop=last and c % 2 == 1, is_transpose=True)
+
+        def fused(t, g):
+            nc.vector.tensor_tensor(g, planes[t][:].indirect(lists[0][:]), wrow[:], ALU.mult)
+
+        def weigh(u, l, c0, nch, ys, g, last):
             n = P * nch
-            per = min(nch, 2)
-            for e in es:
-                t = 2 * u + e
-                for l in range(3):
-                    g = dsts[3 * e + l]()
-                    if (t, l) not in plain:
-                        nc.vector.tensor_tensor(g, planes[t][:].indirect(lists[l][:, 8 * c0:8 * (c0 + nch)]),
-                                                wrow[l][:, P * c0:P * c0 + n], ALU.mult)
-                    elif l < 2:
-                        nc.vector.tensor_tensor(g, plain[(t, l)][:, P * c0:P * c0 + n], wrow[l][:, P * c0:P * c0 + n], ALU.mult)
-                    else:
-                        nc.vector.tensor_tensor(g.rearrange("p (n c) -> p n c", c=4),
-                                                plain[(t, l)][:, P * c0:P * c0 + n].rearrange("p (n c) -> p n c", c=4),
-                                                wbank[2][:, 32 * c0:32 * (c0 + nch), :], ALU.mult)
-                    for c in range(nch):
-                        col = 256 * (c % 2) + P * e
-                        nc.tensor.matmul(ys[c // 2][:, col:col + P], g[:, P * c:P * (c + 1)], ident[:],
-                                         start=(e == 0 and l == 0 and c % 2 == 0),
-                                         stop=(e == 1 and l == 2 and c % 2 == per - 1), is_transpose=True)
+            nc.vector.tensor_tensor(g.rearrange("p (e n c) -> p e n c", e=2, c=4),
+                                    plain[(u, l, c0)][:].rearrange("p e (n c) -> p e n c", c=4),
+                                    wbank[l][:, 32 * c0:32 * (c0 + nch), :].unsqueeze(1).to_broadcast([P, 2, 32 * nch, 4]),
+                                    ALU.mult)
+            for e in range(2):
+                add_up(g[:, n * e:n * (e + 1)], e, nch, ys, False, last and e == 1)
 
-        def ring(n, tags):
-            return [lambda tag=tag: sb([P, n], F32, tag)[:] for tag in tags]
-
-        def parts(tag, k, n):
-            whole = sb([P, k * n], F32, tag)
-            return [lambda i=i: whole[:, n * i:n * (i + 1)] for i in range(k)]
-
-        def turn(y, nch, u, zs, words):
+        def turn(y, nch, u, words, copy):
             xb = words.bitcast(BF16).rearrange("i (c p e) -> i c p e", c=nch, e=2)
-            nc.scalar.copy(out=xb, in_=y[:, 0:256 * nch].rearrange("i (c e p) -> i c p e", c=nch, e=2))
-            return lambda: back(nch, u, zs, words)
+            copy(out=xb, in_=y[:, 0:256 * nch].rearrange("i (c e p) -> i c p e", c=nch, e=2))
 
         def back(nch, u, zs, words):
             for c in range(nch):
@@ -153,11 +152,6 @@ def tile_attend_threenn_kernel(tc, coarse, wa, wb, wc, wf, skip_words, skip_scal
             nc.vector.quantize_mx(out=xc[:].bitcast(FP8X4), scales=xs[:], in_=xg)
             return xc, xs
 
-        def gather_skip(table, h, dtype, tag):
-            g = sb([P, 256], dtype, tag)
-            nc.vector.tensor_copy(g[:], table[:].indirect(lists[3][:, 16 * h:16 * (h + 1)]))
-            return g
-
         def product(dst, n, j, q, o, width, start, stop):
             fc = slice(P * j, P * (j + 1))
             nc.tensor.matmul_mx(out=dst, lhsT=codes[n][:, fc].bitcast(FP8X4), lhsT_scale=scal[n][:, fc],
@@ -173,52 +167,78 @@ def tile_attend_threenn_kernel(tc, coarse, wa, wb, wc, wf, skip_words, skip_scal
 
         oview = out.rearrange("(j p) i -> p j i", p=P)
 
+        obs = {}
+
+        def products(n, h, half, q, o):
+            for jj in range(2):
+                product(obs[(h, half)][:, 256 * jj:256 * (jj + 1)], n, 2 * half + jj, q, o, 256,
+                        n == "ws" and jj == 0, n == "wf" and jj == 1)
+
+        def finish(h, half, engine):
+            o = sb([P, 2, 256], F32, "o%d%d" % (h, half))
+            for jj in range(2):
+                relu(engine, o[:, jj, :], obs[(h, half)][:, 256 * jj:256 * (jj + 1)], 2 * half + jj)
+            nc.sync.dma_start(out=oview[:, 2 * half:2 * half + 2, 256 * h:256 * (h + 1)], in_=o[:])
+
+        def buf(n, tag):
+            return sb([P, n], F32, tag)[:]
+
+        gather_plain(0, 1, 0, 4, "wcol0")
+        gather_plain(0, 2, 0, 4, "wcol1")
+        gather_plain(1, 1, 0, 2, "wcol2")
+        gather_plain(1, 2, 0, 2, "pa")
+        gather_plain(1, 1, 2, 2, "pb")
+        gather_plain(1, 2, 2, 2, "pc")
+        first = buf(4 * NI, "first")
+        for t in range(4):
+            fused(t, first[:, NI * t:NI * (t + 1)])
+        interleave("ws")
+        interleave("wf")
         y0 = [bank(0), bank(1)]
-        weighted(0, 0, 4, y0, ring(NI, ("r0", "r1", "r2", "r0", "r1", "r2")))
-        interleave("wf", 0)
-        interleave("wf", 1)
-        za = bank(4)
-        zb = bank(5)
-        zs = [za[:, 0:256], za[:, 256:512], zb[:, 0:256], zb[:, 256:512]]
-        ya = bank(2)
-        weighted(1, 0, 2, [ya], ring(256, ("r0", "r1", "r2", "r0", "r1", "r2")))
-        quant_w("wf", "r0")
-        mid = sb([P, 4 * P], F32, "raw_wf1")
-        turn(y0[0], 2, 0, zs[0:2], mid[:, 0:2 * P])()
-        turn(ya, 2, 1, zs[0:2], mid[:, 2 * P:4 * P])()
-        interleave("ws", 0)
-        xga = weave(2, za[:], sb([P, 4 * P], F32, "xga")[:])
-        turn(y0[1], 2, 0, zs[2:4], sb([P, 2 * P], F32, "raw_ws0")[:])()
-        yb = bank(3)
-        four = parts("grp_wf", 4, 256)
-        weighted(1, 2, 2, [yb], four[0:3] + ring(256, ("r1", "r2")) + four[3:4], (0,))
-        xq = [quant_x("a", 2, xga)]
-        weighted(1, 2, 2, [yb], four[0:3] + ring(256, ("r1", "r2")) + four[3:4], (1,))
-        obs = [[bank(6), bank(0)], [bank(2), bank(1)]]
-
-        def products(n, h, q):
-            for j in range(4):
-                product(obs[h][j // 2][:, 256 * (j % 2):256 * (j % 2 + 1)], n, j, q, 0, 256,
-                        n == "wf" and j % 2 == 0, n == "ws" and j % 2 == 1)
-
-        def finish(h, engines):
-            o = sb([P, 4, 256], F32, "o%d" % h)
-            for j in range(4):
-                relu(engines[j], o[:, j, :], obs[h][j // 2][:, 256 * (j % 2):256 * (j % 2 + 1)], j)
-                if j % 2 == 1:
-                    nc.sync.dma_start(out=oview[:, j - 1:j + 1, 256 * h:256 * (h + 1)], in_=o[:, j - 1:j + 1, :])
-
-        products("wf", 0, xq[0])
-        sq0 = (gather_skip(sk_w, 0, U16, "r1"), gather_skip(sk_s, 0, U8, "r2"))
-        interleave("ws", 1)
-        turn(yb, 2, 1, zs[2:4], sb([P, 2 * P], F32, "raw_ws1")[:])()
-        xgb = weave(2, zb[:], sb([P, 4 * P], F32, "xgb")[:])
-        quant_w("ws", "grp_wf")
-        products("ws", 0, sq0)
-        w1 = gather_skip(sk_w, 1, U16, "grp_ws")
-        xq.append(quant_x("b", 2, xgb))
-        products("wf", 1, xq[1])
-        sq1 = (w1, gather_skip(sk_s, 1, U8, "xgb"))
-        finish(0, "ssss")
-        products("ws", 1, sq1)
-        finish(1, "vvss")
+        for e in range(2):
+            add_up(first[:, NI * e:NI * (e + 1)], e, 4, y0, e == 0, False)
+        weigh(0, 1, 0, 4, y0, buf(2 * NI, "plane0"), False)
+        weigh(0, 2, 0, 4, y0, buf(2 * NI, "plane1"), True)
+        ya, yb = [bank(2)], [bank(3)]
+        for h, y in enumerate((ya, yb)):
+            for e in range(2):
+                o = NI * (2 + e) + 256 * h
+                add_up(first[:, o:o + 256], e, 2, y, e == 0, False)
+        weigh(1, 1, 0, 2, ya, buf(NI, "wcol0"), False)
+        weigh(1, 2, 0, 2, ya, buf(NI, "wcol1"), True)
+        quant_w("ws", "wcol2")
+        picked_w = sb([P, NI], U16, "pa")
+        nc.vector.tensor_copy(picked_w[:], sk_w[:].indirect(lists[3][:]))
+        skip = (picked_w, sk_plane)
+        obs[(0, 0)], obs[(0, 1)] = bank(4), bank(6)
+        products("ws", 0, 0, skip, 0)
+        products("ws", 0, 1, skip, 0)
+        weigh(1, 1, 2, 2, yb, buf(NI, "grp_ws"), False)
+        weigh(1, 2, 2, 2, yb, buf(NI, "plane0"), True)
+        pairs = buf(8 * P, "plane2")
+        turn(y0[0], 2, 0, pairs[:, 0:256], nc.scalar.copy)
+        turn(ya[0], 2, 1, pairs[:, 256:512], nc.scalar.copy)
+        za = bank(2)
+        back(2, 0, [za[:, 0:256], za[:, 256:512]], pairs[:, 0:256])
+        back(2, 1, [za[:, 0:256], za[:, 256:512]], pairs[:, 256:512])
+        turn(y0[1], 2, 0, pairs[:, 512:768], nc.scalar.copy)
+        xga = weave(2, za[:], buf(4 * P, "xga"))
+        quant_w("wf", "pb")
+        turn(yb[0], 2, 1, pairs[:, 768:1024], nc.vector.tensor_copy)
+        obs[(1, 0)], obs[(1, 1)] = bank(0), bank(1)
+        products("ws", 1, 0, skip, 256)
+        zb = bank(3)
+        back(2, 0, [zb[:, 0:256], zb[:, 256:512]], pairs[:, 512:768])
+        back(2, 1, [zb[:, 0:256], zb[:, 256:512]], pairs[:, 768:1024])
+        products("ws", 1, 1, skip, 256)
+        xqa = quant_x("a", 2, xga)
+        xgb = weave(2, zb[:], buf(4 * P, "xgb"))
+        products("wf", 0, 0, xqa, 0)
+        products("wf", 0, 1, xqa, 0)
+        xqb = quant_x("b", 2, xgb)
+        finish(0, 0, "s")
+        finish(0, 1, "v")
+        products("wf", 1, 0, xqb, 0)
+        products("wf", 1, 1, xqb, 0)
+        finish(1, 0, "s")
+        finish(1, 1, "v")

@@ -44,7 +44,7 @@ def tile_attend_threenn_kernel(tc, coarse, wa, wb, wc, wf, skip_words, skip_scal
         sk_s = sb([P, T], U8, "sk_s")
         raw = {n: [sb([P, 4, F // 2], F32, "raw_%s%d" % (n, h)) for h in range(2)] for n in ("wf", "ws")}
         scal = {n: sb([P, F], U8, "scal_" + n) for n in ("wf", "ws")}
-        grp = {n: sb([P, F, 4], BF16, "grp_" + n) for n in ("wf", "ws")}
+        grp = {}
         codes = {}
         wrow = sb([P, NI], F32, "wrow")
 
@@ -65,12 +65,12 @@ def tile_attend_threenn_kernel(tc, coarse, wa, wb, wc, wf, skip_words, skip_scal
         load_col(0)
         nc.sync.dma_start(out=sk_s[:].bitcast(I32)[112:128, :], in_=skip_scales[0].bitcast(I32))
         nc.sync.dma_start(lists[3][:], offs4)
-        load_col(1)
-        nc.sync.dma_start(lists[0][:], offs)
-        nc.sync.dma_start(lists[2][:], offs3)
-        load_col(2)
         nc.sync.dma_start(out=planes[0][:], in_=cview[:, 0, :])
+        nc.sync.dma_start(lists[0][:], offs)
         nc.sync.dma_start(lists[1][:], offs2)
+        load_col(1)
+        load_col(2)
+        nc.sync.dma_start(lists[2][:], offs3)
         for t in range(1, 4):
             nc.sync.dma_start(out=planes[t][:], in_=cview[:, t, :])
         load_w("ws", 0)
@@ -91,9 +91,9 @@ def tile_attend_threenn_kernel(tc, coarse, wa, wb, wc, wf, skip_words, skip_scal
         for l in range(3):
             b = bank((4, 5, 7)[l])
             for c in range(4):
-                nc.tensor.transpose(b[:, P * c:P * (c + 1)], wcol[l][:, c:c + 1].to_broadcast([P, P]), ident[:])
-            wbank.append(b[:].rearrange("p (c n) -> p n c", c=4))
-        nc.scalar.copy(out=wrow[:].rearrange("p (n c) -> p n c", c=4), in_=wbank[0])
+                nc.tensor.transpose(b[:].rearrange("p (n c) -> p c n", c=4)[:, c, :], wcol[l][:, c:c + 1].to_broadcast([P, P]), ident[:])
+            wbank.append(b)
+        nc.scalar.copy(out=wrow[:], in_=wbank[0][:])
 
         plain = {}
 
@@ -103,7 +103,8 @@ def tile_attend_threenn_kernel(tc, coarse, wa, wb, wc, wf, skip_words, skip_scal
                 nc.scalar.activation(out=g[:, e, :], in_=planes[2 * u + e][:].indirect(lists[l][:, 8 * c0:8 * (c0 + nch)]),
                                      func=ACT.Copy)
 
-        def interleave(n):
+        def interleave(n, tag):
+            grp[n] = sb([P, F, 4], BF16, tag)
             for j in range(4):
                 src = raw[n][j // 2][:, :, P * (j % 2):P * (j % 2 + 1)].rearrange("p t f -> p f t")
                 nc.gpsimd.tensor_scalar(out=grp[n][:, P * j:P * (j + 1), :], in0=src, scalar1=1.0, scalar2=0.0,
@@ -125,10 +126,8 @@ def tile_attend_threenn_kernel(tc, coarse, wa, wb, wc, wf, skip_words, skip_scal
 
         def weigh(u, l, c0, nch, ys, g, last):
             n = P * nch
-            nc.vector.tensor_tensor(g.rearrange("p (e n c) -> p e n c", e=2, c=4),
-                                    plain[(u, l, c0)][:].rearrange("p e (n c) -> p e n c", c=4),
-                                    wbank[l][:, 32 * c0:32 * (c0 + nch), :].unsqueeze(1).to_broadcast([P, 2, 32 * nch, 4]),
-                                    ALU.mult)
+            nc.vector.tensor_tensor(g.rearrange("p (e n) -> p e n", e=2), plain[(u, l, c0)][:],
+                                    wbank[l][:, P * c0:P * c0 + n].unsqueeze(1).to_broadcast([P, 2, n]), ALU.mult)
             for e in range(2):
                 add_up(g[:, n * e:n * (e + 1)], e, nch, ys, False, last and e == 1)
 
@@ -192,8 +191,7 @@ def tile_attend_threenn_kernel(tc, coarse, wa, wb, wc, wf, skip_words, skip_scal
         first = buf(4 * NI, "first")
         for t in range(4):
             fused(t, first[:, NI * t:NI * (t + 1)])
-        interleave("ws")
-        interleave("wf")
+        interleave("ws", "wrow")
         y0 = [bank(0), bank(1)]
         for e in range(2):
             add_up(first[:, NI * e:NI * (e + 1)], e, 4, y0, e == 0, False)
@@ -205,15 +203,16 @@ def tile_attend_threenn_kernel(tc, coarse, wa, wb, wc, wf, skip_words, skip_scal
                 o = NI * (2 + e) + 256 * h
                 add_up(first[:, o:o + 256], e, 2, y, e == 0, False)
         weigh(1, 1, 0, 2, ya, buf(NI, "wcol0"), False)
-        weigh(1, 2, 0, 2, ya, buf(NI, "wcol1"), True)
         quant_w("ws", "wcol2")
+        interleave("wf", "wrow")
+        weigh(1, 2, 0, 2, ya, buf(NI, "wcol1"), True)
         picked_w = sb([P, NI], U16, "pa")
         nc.vector.tensor_copy(picked_w[:], sk_w[:].indirect(lists[3][:]))
         skip = (picked_w, sk_plane)
         obs[(0, 0)], obs[(0, 1)] = bank(4), bank(6)
         products("ws", 0, 0, skip, 0)
         products("ws", 0, 1, skip, 0)
-        weigh(1, 1, 2, 2, yb, buf(NI, "grp_ws"), False)
+        weigh(1, 1, 2, 2, yb, buf(NI, "plane1"), False)
         weigh(1, 2, 2, 2, yb, buf(NI, "plane0"), True)
         pairs = buf(8 * P, "plane2")
         turn(y0[0], 2, 0, pairs[:, 0:256], nc.scalar.copy)

@@ -174,10 +174,11 @@ def tile_attend_threenn_kernel(tc, coarse, wa, wb, wc, wf, skip_words, skip_scal
                         n == "ws" and jj == 0, n == "wf" and jj == 1)
 
         def finish(h, half, engine):
-            o = sb([P, 2, 256], F32, "o%d%d" % (h, half))
             for jj in range(2):
-                relu(engine, o[:, jj, :], obs[(h, half)][:, 256 * jj:256 * (jj + 1)], 2 * half + jj)
-            nc.sync.dma_start(out=oview[:, 2 * half:2 * half + 2, 256 * h:256 * (h + 1)], in_=o[:])
+                j = 2 * half + jj
+                o = buf(256, "o%d%d" % (h, j))
+                relu(engine, o, obs[(h, half)][:, 256 * jj:256 * (jj + 1)], j)
+                nc.sync.dma_start(out=oview[:, j, 256 * h:256 * (h + 1)], in_=o)
 
         def buf(n, tag):
             return sb([P, n], F32, tag)[:]
@@ -202,34 +203,44 @@ def tile_attend_threenn_kernel(tc, coarse, wa, wb, wc, wf, skip_words, skip_scal
             for e in range(2):
                 o = NI * (2 + e) + 256 * h
                 add_up(first[:, o:o + 256], e, 2, y, e == 0, False)
-        weigh(1, 1, 0, 2, ya, buf(NI, "wcol0"), False)
+        skip = []
+
+        def gather_words(h, tag):
+            g = sb([P, 256], U16, tag)
+            nc.vector.tensor_copy(g[:], sk_w[:].indirect(lists[3][:, 16 * h:16 * (h + 1)]))
+            skip.append((g, sk_plane[:, 256 * h:256 * (h + 1)]))
+
+        gather_words(0, "wcol0")
+        weigh(1, 1, 0, 2, ya, buf(NI, "wcol1"), False)
         quant_w("ws", "wcol2")
         interleave("wf", "wrow")
-        weigh(1, 2, 0, 2, ya, buf(NI, "wcol1"), True)
-        picked_w = sb([P, NI], U16, "pa")
-        nc.vector.tensor_copy(picked_w[:], sk_w[:].indirect(lists[3][:]))
-        skip = (picked_w, sk_plane)
         obs[(0, 0)], obs[(0, 1)] = bank(4), bank(6)
-        products("ws", 0, 0, skip, 0)
-        products("ws", 0, 1, skip, 0)
-        weigh(1, 1, 2, 2, yb, buf(NI, "plane1"), False)
-        weigh(1, 2, 2, 2, yb, buf(NI, "plane0"), True)
+        products("ws", 0, 0, skip[0], 0)
+        weigh(1, 2, 0, 2, ya, buf(NI, "plane0"), True)
+        products("ws", 0, 1, skip[0], 0)
+        gather_words(1, "pa")
         pairs = buf(8 * P, "plane2")
         turn(y0[0], 2, 0, pairs[:, 0:256], nc.scalar.copy)
+        ends = {0: bank(0)}
+        product(ends[0][:, 0:256], "ws", 0, skip[1], 0, 256, True, False)
+        weigh(1, 1, 2, 2, yb, buf(NI, "plane1"), False)
+        ends[1] = bank(5)
+        product(ends[1][:, 0:256], "ws", 1, skip[1], 0, 256, True, False)
+        weigh(1, 2, 2, 2, yb, buf(NI, "plane0"), True)
         turn(ya[0], 2, 1, pairs[:, 256:512], nc.scalar.copy)
         za = bank(2)
         back(2, 0, [za[:, 0:256], za[:, 256:512]], pairs[:, 0:256])
         back(2, 1, [za[:, 0:256], za[:, 256:512]], pairs[:, 256:512])
         turn(y0[1], 2, 0, pairs[:, 512:768], nc.scalar.copy)
         xga = weave(2, za[:], buf(4 * P, "xga"))
-        quant_w("wf", "pb")
         turn(yb[0], 2, 1, pairs[:, 768:1024], nc.vector.tensor_copy)
-        obs[(1, 0)], obs[(1, 1)] = bank(0), bank(1)
-        products("ws", 1, 0, skip, 256)
+        quant_w("wf", "plane0")
         zb = bank(3)
         back(2, 0, [zb[:, 0:256], zb[:, 256:512]], pairs[:, 512:768])
         back(2, 1, [zb[:, 0:256], zb[:, 256:512]], pairs[:, 768:1024])
-        products("ws", 1, 1, skip, 256)
+        ends[2], ends[3] = bank(1), bank(7)
+        for j in (2, 3):
+            product(ends[j][:, 0:256], "ws", j, skip[1], 0, 256, True, False)
         xqa = quant_x("a", 2, xga)
         xgb = weave(2, zb[:], buf(4 * P, "xgb"))
         products("wf", 0, 0, xqa, 0)
@@ -237,7 +248,8 @@ def tile_attend_threenn_kernel(tc, coarse, wa, wb, wc, wf, skip_words, skip_scal
         xqb = quant_x("b", 2, xgb)
         finish(0, 0, "s")
         finish(0, 1, "v")
-        products("wf", 1, 0, xqb, 0)
-        products("wf", 1, 1, xqb, 0)
-        finish(1, 0, "s")
-        finish(1, 1, "v")
+        for j in range(4):
+            product(ends[j][:, 0:256], "wf", j, xqb, 0, 256, False, True)
+            o = buf(256, "o1%d" % j)
+            relu("svsv"[j], o, ends[j][:, 0:256], j)
+            nc.sync.dma_start(out=oview[:, j, 256:512], in_=o)

@@ -76,16 +76,15 @@ def tile_attend_threenn_kernel(tc, coarse, wa, wb, wc, wf, skip_words, skip_scal
         load_w("ws", 0)
         load_w("ws", 1)
         nc.sync.dma_start(out=sk_w[:].bitcast(I32), in_=skip_words[0].bitcast(I32))
-        load_w("wf", 0)
-        load_w("wf", 1)
-        with nc.allow_non_contiguous_dma(reason="one bias value a partition"):
-            nc.sync.dma_start(out=bcol[:], in_=bias.rearrange("(j p) o -> p (j o)", p=P))
-
         picked = sb([P, NI], U8, "picked")
         nc.vector.tensor_copy(picked[:], sk_s[:].indirect(lists[3][:]))
         for q in range(4):
             nc.sync.dma_start(out=sk_plane[:].bitcast(I32)[32 * q:32 * q + 4, :],
                               in_=picked[:].bitcast(I32)[112 + 4 * q:116 + 4 * q, :])
+        load_w("wf", 0)
+        load_w("wf", 1)
+        with nc.allow_non_contiguous_dma(reason="one bias value a partition"):
+            nc.sync.dma_start(out=bcol[:], in_=bias.rearrange("(j p) o -> p (j o)", p=P))
 
         wbank = []
         for l in range(3):
@@ -219,25 +218,26 @@ def tile_attend_threenn_kernel(tc, coarse, wa, wb, wc, wf, skip_words, skip_scal
         weigh(1, 2, 0, 2, ya, buf(NI, "plane0"), True)
         products("ws", 0, 1, skip[0], 0)
         gather_words(1, "pa")
-        pairs = buf(8 * P, "plane2")
+        pairs = buf(4 * P, "plane2")
         turn(y0[0], 2, 0, pairs[:, 0:256], nc.scalar.copy)
-        ends = {0: bank(0)}
-        product(ends[0][:, 0:256], "ws", 0, skip[1], 0, 256, True, False)
         weigh(1, 1, 2, 2, yb, buf(NI, "plane1"), False)
-        ends[1] = bank(5)
+        ends = {1: bank(5)}
         product(ends[1][:, 0:256], "ws", 1, skip[1], 0, 256, True, False)
         weigh(1, 2, 2, 2, yb, buf(NI, "plane0"), True)
         turn(ya[0], 2, 1, pairs[:, 256:512], nc.scalar.copy)
         za = bank(2)
         back(2, 0, [za[:, 0:256], za[:, 256:512]], pairs[:, 0:256])
         back(2, 1, [za[:, 0:256], za[:, 256:512]], pairs[:, 256:512])
-        turn(y0[1], 2, 0, pairs[:, 512:768], nc.scalar.copy)
+        ends[0] = bank(0)
+        product(ends[0][:, 0:256], "ws", 0, skip[1], 0, 256, True, False)
+        pairs_b = buf(4 * P, "pc")
+        turn(y0[1], 2, 0, pairs_b[:, 0:256], nc.vector.tensor_copy)
+        turn(yb[0], 2, 1, pairs_b[:, 256:512], nc.vector.tensor_copy)
         xga = weave(2, za[:], buf(4 * P, "xga"))
-        turn(yb[0], 2, 1, pairs[:, 768:1024], nc.vector.tensor_copy)
         quant_w("wf", "plane0")
         zb = bank(3)
-        back(2, 0, [zb[:, 0:256], zb[:, 256:512]], pairs[:, 512:768])
-        back(2, 1, [zb[:, 0:256], zb[:, 256:512]], pairs[:, 768:1024])
+        back(2, 0, [zb[:, 0:256], zb[:, 256:512]], pairs_b[:, 0:256])
+        back(2, 1, [zb[:, 0:256], zb[:, 256:512]], pairs_b[:, 256:512])
         ends[2], ends[3] = bank(1), bank(7)
         for j in (2, 3):
             product(ends[j][:, 0:256], "ws", j, skip[1], 0, 256, True, False)
@@ -247,9 +247,9 @@ def tile_attend_threenn_kernel(tc, coarse, wa, wb, wc, wf, skip_words, skip_scal
         products("wf", 0, 1, xqa, 0)
         xqb = quant_x("b", 2, xgb)
         finish(0, 0, "s")
-        finish(0, 1, "v")
+        finish(0, 1, "s")
         for j in range(4):
             product(ends[j][:, 0:256], "wf", j, xqb, 0, 256, False, True)
             o = buf(256, "o1%d" % j)
-            relu("svsv"[j], o, ends[j][:, 0:256], j)
-            nc.sync.dma_start(out=oview[:, j, 256:512], in_=o)
+            relu("vvsv"[j], o, ends[j][:, 0:256], j)
+            (nc.scalar if j == 2 else nc.sync).dma_start(out=oview[:, j, 256:512], in_=o)

@@ -78,21 +78,22 @@ def tile_attend_threenn_kernel(tc, coarse, wa, wb, wc, wf, skip_words, skip_scal
         nc.sync.dma_start(out=sk_w[:].bitcast(I32), in_=skip_words[0].bitcast(I32))
         picked = sb([P, NI], U8, "picked")
         nc.vector.tensor_copy(picked[:], sk_s[:].indirect(lists[3][:]))
-        for q in range(4):
-            nc.sync.dma_start(out=sk_plane[:].bitcast(I32)[32 * q:32 * q + 4, :],
-                              in_=picked[:].bitcast(I32)[112 + 4 * q:116 + 4 * q, :])
         load_w("wf", 0)
         load_w("wf", 1)
         with nc.allow_non_contiguous_dma(reason="one bias value a partition"):
             nc.sync.dma_start(out=bcol[:], in_=bias.rearrange("(j p) o -> p (j o)", p=P))
 
+        for q in range(4):
+            nc.sync.dma_start(out=sk_plane[:].bitcast(I32)[32 * q:32 * q + 4, :],
+                              in_=picked[:].bitcast(I32)[112 + 4 * q:116 + 4 * q, :])
+
         wbank = []
         for l in range(3):
             b = bank((4, 5, 7)[l])
             for c in range(4):
-                nc.tensor.transpose(b[:].rearrange("p (n c) -> p c n", c=4)[:, c, :], wcol[l][:, c:c + 1].to_broadcast([P, P]), ident[:])
+                nc.tensor.transpose(b[:].rearrange("p (c n) -> p c n" if l == 0 else "p (n c) -> p c n", c=4)[:, c, :], wcol[l][:, c:c + 1].to_broadcast([P, P]), ident[:])
             wbank.append(b)
-        nc.scalar.copy(out=wrow[:], in_=wbank[0][:])
+        nc.scalar.copy(out=wrow[:].rearrange("p (n c) -> p n c", c=4), in_=wbank[0][:].rearrange("p (c n) -> p n c", c=4))
 
         plain = {}
 
@@ -104,10 +105,9 @@ def tile_attend_threenn_kernel(tc, coarse, wa, wb, wc, wf, skip_words, skip_scal
 
         def interleave(n, tag):
             grp[n] = sb([P, F, 4], BF16, tag)
-            for j in range(4):
-                src = raw[n][j // 2][:, :, P * (j % 2):P * (j % 2 + 1)].rearrange("p t f -> p f t")
-                nc.gpsimd.tensor_scalar(out=grp[n][:, P * j:P * (j + 1), :], in0=src, scalar1=1.0, scalar2=0.0,
-                                        op0=ALU.mult, op1=ALU.add)
+            for h in range(2):
+                nc.gpsimd.tensor_scalar(out=grp[n][:, 256 * h:256 * (h + 1), :], in0=raw[n][h][:].rearrange("p t f -> p f t"),
+                                        scalar1=1.0, scalar2=0.0, op0=ALU.mult, op1=ALU.add)
 
         def quant_w(n, tag):
             codes[n] = sb([P, F], U32, tag)

@@ -177,7 +177,8 @@ def tile_attend_threenn_kernel(tc, coarse, wa, wb, wc, wf, skip_words, skip_scal
                 j = 2 * half + jj
                 o = buf(256, "o%d%d" % (h, j))
                 relu(engine, o, obs[(h, half)][:, 256 * jj:256 * (jj + 1)], j)
-                nc.sync.dma_start(out=oview[:, j, 256 * h:256 * (h + 1)], in_=o)
+                queue = nc.scalar if (h, j) == (1, 1) else nc.sync
+                queue.dma_start(out=oview[:, j, 256 * h:256 * (h + 1)], in_=o)
 
         def buf(n, tag):
             return sb([P, n], F32, tag)[:]
@@ -215,41 +216,41 @@ def tile_attend_threenn_kernel(tc, coarse, wa, wb, wc, wf, skip_words, skip_scal
         interleave("wf", "wrow")
         obs[(0, 0)], obs[(0, 1)] = bank(4), bank(6)
         products("ws", 0, 0, skip[0], 0)
-        weigh(1, 2, 0, 2, ya, buf(NI, "plane0"), True)
         products("ws", 0, 1, skip[0], 0)
+        weigh(1, 2, 0, 2, ya, buf(NI, "plane0"), True)
         gather_words(1, "pa")
         pairs = buf(4 * P, "plane2")
         turn(y0[0], 2, 0, pairs[:, 0:256], nc.scalar.copy)
         weigh(1, 1, 2, 2, yb, buf(NI, "plane1"), False)
-        ends = {1: bank(5)}
-        product(ends[1][:, 0:256], "ws", 1, skip[1], 0, 256, True, False)
         weigh(1, 2, 2, 2, yb, buf(NI, "plane0"), True)
         turn(ya[0], 2, 1, pairs[:, 256:512], nc.scalar.copy)
-        za = bank(2)
+        za = bank(5)
         back(2, 0, [za[:, 0:256], za[:, 256:512]], pairs[:, 0:256])
         back(2, 1, [za[:, 0:256], za[:, 256:512]], pairs[:, 256:512])
-        ends[0] = bank(0)
-        product(ends[0][:, 0:256], "ws", 0, skip[1], 0, 256, True, False)
         pairs_b = buf(4 * P, "pc")
         turn(y0[1], 2, 0, pairs_b[:, 0:256], nc.vector.tensor_copy)
         turn(yb[0], 2, 1, pairs_b[:, 256:512], nc.vector.tensor_copy)
         xga = weave(2, za[:], buf(4 * P, "xga"))
         quant_w("wf", "plane0")
-        zb = bank(3)
+        zb = bank(7)
         back(2, 0, [zb[:, 0:256], zb[:, 256:512]], pairs_b[:, 0:256])
         back(2, 1, [zb[:, 0:256], zb[:, 256:512]], pairs_b[:, 256:512])
-        ends[2], ends[3] = bank(1), bank(7)
-        for j in (2, 3):
-            product(ends[j][:, 0:256], "ws", j, skip[1], 0, 256, True, False)
+        obs[(1, 0)] = bank(3)
+        products("ws", 1, 0, skip[1], 0)
         xqa = quant_x("a", 2, xga)
         xgb = weave(2, zb[:], buf(4 * P, "xgb"))
         products("wf", 0, 0, xqa, 0)
         products("wf", 0, 1, xqa, 0)
         xqb = quant_x("b", 2, xgb)
         finish(0, 0, "s")
-        finish(0, 1, "s")
-        for j in range(4):
+        finish(0, 1, "v")
+        ends = {2: bank(5), 3: bank(7)}
+        product(ends[2][:, 0:256], "ws", 2, skip[1], 0, 256, True, False)
+        products("wf", 1, 0, xqb, 0)
+        finish(1, 0, "s")
+        product(ends[3][:, 0:256], "ws", 3, skip[1], 0, 256, True, False)
+        for j in (2, 3):
             product(ends[j][:, 0:256], "wf", j, xqb, 0, 256, False, True)
             o = buf(256, "o1%d" % j)
-            relu("vvsv"[j], o, ends[j][:, 0:256], j)
-            (nc.scalar if j == 2 else nc.sync).dma_start(out=oview[:, j, 256:512], in_=o)
+            relu("v", o, ends[j][:, 0:256], j)
+            nc.sync.dma_start(out=oview[:, j, 256:512], in_=o)

@@ -69,9 +69,10 @@ def tile_attend_threenn_kernel(tc, coarse, wa, wb, wc, wf, skip_words, skip_scal
         nc.sync.dma_start(lists[0][:], offs)
         nc.sync.dma_start(lists[1][:], offs2)
         load_col(1)
+        nc.sync.dma_start(out=planes[1][:], in_=cview[:, 1, :])
         load_col(2)
         nc.sync.dma_start(lists[2][:], offs3)
-        for t in range(1, 4):
+        for t in (2, 3):
             nc.sync.dma_start(out=planes[t][:], in_=cview[:, t, :])
         load_w("ws", 0)
         load_w("ws", 1)
@@ -245,10 +246,10 @@ def tile_attend_threenn_kernel(tc, coarse, wa, wb, wc, wf, skip_words, skip_scal
         finish(0, 0, "s")
         finish(0, 1, "v")
         ends = {2: bank(5), 3: bank(7)}
-        product(ends[2][:, 0:256], "ws", 2, skip[1], 0, 256, True, False)
+        for j in (2, 3):
+            product(ends[j][:, 0:256], "ws", j, skip[1], 0, 256, True, False)
         products("wf", 1, 0, xqb, 0)
         finish(1, 0, "s")
-        product(ends[3][:, 0:256], "ws", 3, skip[1], 0, 256, True, False)
         for j in (2, 3):
             product(ends[j][:, 0:256], "wf", j, xqb, 0, 256, False, True)
             o = buf(256, "o1%d" % j)

@@ -81,12 +81,12 @@ def tile_attend_threenn_kernel(tc, coarse, wa, wb, wc, wf, skip_words, skip_scal
         nc.vector.tensor_copy(picked[:], sk_s[:].indirect(lists[3][:]))
         load_w("wf", 0)
         load_w("wf", 1)
-        with nc.allow_non_contiguous_dma(reason="one bias value a partition"):
-            nc.sync.dma_start(out=bcol[:], in_=bias.rearrange("(j p) o -> p (j o)", p=P))
 
         for q in range(4):
             nc.sync.dma_start(out=sk_plane[:].bitcast(I32)[32 * q:32 * q + 4, :],
                               in_=picked[:].bitcast(I32)[112 + 4 * q:116 + 4 * q, :])
+        with nc.allow_non_contiguous_dma(reason="one bias value a partition"):
+            nc.sync.dma_start(out=bcol[:], in_=bias.rearrange("(j p) o -> p (j o)", p=P))
 
         wbank = []
         for l in range(3):
@@ -228,14 +228,14 @@ def tile_attend_threenn_kernel(tc, coarse, wa, wb, wc, wf, skip_words, skip_scal
         za = bank(5)
         back(2, 0, [za[:, 0:256], za[:, 256:512]], pairs[:, 0:256])
         back(2, 1, [za[:, 0:256], za[:, 256:512]], pairs[:, 256:512])
-        pairs_b = buf(4 * P, "pc")
-        turn(y0[1], 2, 0, pairs_b[:, 0:256], nc.vector.tensor_copy)
-        turn(yb[0], 2, 1, pairs_b[:, 256:512], nc.vector.tensor_copy)
+        pairs_b = [buf(2 * P, "plane3"), buf(2 * P, "pc")]
+        turn(y0[1], 2, 0, pairs_b[0], nc.scalar.copy)
+        turn(yb[0], 2, 1, pairs_b[1], nc.vector.tensor_copy)
         xga = weave(2, za[:], buf(4 * P, "xga"))
         quant_w("wf", "plane0")
         zb = bank(7)
-        back(2, 0, [zb[:, 0:256], zb[:, 256:512]], pairs_b[:, 0:256])
-        back(2, 1, [zb[:, 0:256], zb[:, 256:512]], pairs_b[:, 256:512])
+        back(2, 0, [zb[:, 0:256], zb[:, 256:512]], pairs_b[0])
+        back(2, 1, [zb[:, 0:256], zb[:, 256:512]], pairs_b[1])
         obs[(1, 0)] = bank(3)
         products("ws", 1, 0, skip[1], 0)
         xqa = quant_x("a", 2, xga)

@@ -83,8 +83,8 @@ def tile_attend_threenn_kernel(tc, coarse, wa, wb, wc, wf, skip_words, skip_scal
         load_w("wf", 1)
 
         for q in range(4):
-            nc.sync.dma_start(out=sk_plane[:].bitcast(I32)[32 * q:32 * q + 4, :],
-                              in_=picked[:].bitcast(I32)[112 + 4 * q:116 + 4 * q, :])
+            nc.gpsimd.dma_start(out=sk_plane[:].bitcast(I32)[32 * q:32 * q + 4, :],
+                                in_=picked[:].bitcast(I32)[112 + 4 * q:116 + 4 * q, :])
         with nc.allow_non_contiguous_dma(reason="one bias value a partition"):
             nc.sync.dma_start(out=bcol[:], in_=bias.rearrange("(j p) o -> p (j o)", p=P))
 
@@ -219,11 +219,11 @@ def tile_attend_threenn_kernel(tc, coarse, wa, wb, wc, wf, skip_words, skip_scal
         products("ws", 0, 0, skip[0], 0)
         products("ws", 0, 1, skip[0], 0)
         weigh(1, 2, 0, 2, ya, buf(NI, "plane0"), True)
-        gather_words(1, "pa")
         pairs = buf(4 * P, "plane2")
         turn(y0[0], 2, 0, pairs[:, 0:256], nc.scalar.copy)
         weigh(1, 1, 2, 2, yb, buf(NI, "plane1"), False)
-        weigh(1, 2, 2, 2, yb, buf(NI, "plane0"), True)
+        weigh(1, 2, 2, 2, yb, buf(NI, "pa"), True)
+        gather_words(1, "pb")
         turn(ya[0], 2, 1, pairs[:, 256:512], nc.scalar.copy)
         za = bank(5)
         back(2, 0, [za[:, 0:256], za[:, 256:512]], pairs[:, 0:256])
@@ -232,7 +232,7 @@ def tile_attend_threenn_kernel(tc, coarse, wa, wb, wc, wf, skip_words, skip_scal
         turn(y0[1], 2, 0, pairs_b[0], nc.scalar.copy)
         turn(yb[0], 2, 1, pairs_b[1], nc.vector.tensor_copy)
         xga = weave(2, za[:], buf(4 * P, "xga"))
-        quant_w("wf", "plane0")
+        quant_w("wf", "pa")
         zb = bank(7)
         back(2, 0, [zb[:, 0:256], zb[:, 256:512]], pairs_b[0])
         back(2, 1, [zb[:, 0:256], zb[:, 256:512]], pairs_b[1])

@@ -16,6 +16,8 @@ ALU = mybir.AluOpType
 
 P = 128
 K, U, R, T, NI, F = 512, 1024, 512, 2048, 512, 512
+HALF = 2 * P
+SCALE_ROW0 = P - 16
 FLOPS = 2 * (K + R) * NI * F
 
 
@@ -24,12 +26,16 @@ def tile_attend_threenn_kernel(tc, coarse, wa, wb, wc, wf, skip_words, skip_scal
     nc = tc.nc
     with ExitStack() as ctx:
         keep = ctx.enter_context(tc.tile_pool(name="keep", bufs=1))
+        laid = ctx.enter_context(tc.tile_pool(name="laid", bufs=1))
         psum = ctx.enter_context(tc.psum_pool(name="psum", bufs=1))
         made = []
 
         def sb(shape, dtype, tag):
             made.append(tag)
             return keep.tile(shape, dtype, name="%s_%d" % (tag, len(made)), tag=tag, align_bytes=64)
+
+        def buf(n, tag):
+            return sb([P, n], F32, tag)[:]
 
         def bank(b):
             made.append(b)
@@ -42,28 +48,29 @@ def tile_attend_threenn_kernel(tc, coarse, wa, wb, wc, wf, skip_words, skip_scal
         ident = sb([P, P], F32, "ident")
         sk_w = sb([P, T], U16, "sk_w")
         sk_s = sb([P, T], U8, "sk_s")
-        raw = {n: [sb([P, 4, F // 2], F32, "raw_%s%d" % (n, h)) for h in range(2)] for n in ("wf", "ws")}
+        raw = {n: sb([P, 4, F], F32, "raw_" + n) for n in ("wf", "ws")}
         scal = {n: sb([P, F], U8, "scal_" + n) for n in ("wf", "ws")}
-        grp = {}
+        grouped = {}
         codes = {}
-        wrow = sb([P, NI], F32, "wrow")
+        wrow = laid.tile([P, NI], F32, name="wrow", offset=4096, align_bytes=64)
 
         make_identity(nc, ident[:])
         sk_plane = sb([P, NI], U8, "sk_plane")
-        nc.vector.memset(sk_s[:].bitcast(I32)[0:112, :], 0)
+        nc.vector.memset(sk_s[:].bitcast(I32)[0:SCALE_ROW0, :], 0)
         nc.gpsimd.memset(sk_plane[:].bitcast(I32), 0)
 
         cview = coarse.rearrange("(p t) u -> p t u", t=4)
         wview = {"wf": wf.rearrange("(p t) f -> p t f", t=4), "ws": ws.rearrange("(p t) f -> p t f", t=4)}
 
-        def load_w(n, h):
-            nc.sync.dma_start(out=raw[n][h][:], in_=wview[n][:, :, 256 * h:256 * (h + 1)])
+        def load_matrix(n):
+            nc.sync.dma_start(out=raw[n][:], in_=wview[n])
 
         def load_col(l):
             nc.sync.dma_start(out=wcol[l][:], in_=(wa, wb, wc)[l].rearrange("o (p c) -> p (o c)", c=4))
 
-        load_col(0)
-        nc.sync.dma_start(out=sk_s[:].bitcast(I32)[112:128, :], in_=skip_scales[0].bitcast(I32))
+        with nc.allow_non_contiguous_dma(reason="two pairs of weights a partition"):
+            nc.sync.dma_start(out=wcol[0][:].rearrange("p (h c) -> p h c", c=2), in_=wa.rearrange("o (h p c) -> p (o h) c", h=2, c=2))
+        nc.sync.dma_start(out=sk_s[:].bitcast(I32)[SCALE_ROW0:P, :], in_=skip_scales[0].bitcast(I32))
         nc.sync.dma_start(lists[3][:], offs4)
         nc.sync.dma_start(out=planes[0][:], in_=cview[:, 0, :])
         nc.sync.dma_start(lists[0][:], offs)
@@ -74,27 +81,30 @@ def tile_attend_threenn_kernel(tc, coarse, wa, wb, wc, wf, skip_words, skip_scal
         nc.sync.dma_start(lists[2][:], offs3)
         for t in (2, 3):
             nc.sync.dma_start(out=planes[t][:], in_=cview[:, t, :])
-        load_w("ws", 0)
-        load_w("ws", 1)
+        load_matrix("ws")
         nc.sync.dma_start(out=sk_w[:].bitcast(I32), in_=skip_words[0].bitcast(I32))
         picked = sb([P, NI], U8, "picked")
         nc.vector.tensor_copy(picked[:], sk_s[:].indirect(lists[3][:]))
-        load_w("wf", 0)
-        load_w("wf", 1)
+        load_matrix("wf")
 
         for q in range(4):
             nc.gpsimd.dma_start(out=sk_plane[:].bitcast(I32)[32 * q:32 * q + 4, :],
-                                in_=picked[:].bitcast(I32)[112 + 4 * q:116 + 4 * q, :])
+                                in_=picked[:].bitcast(I32)[SCALE_ROW0 + 4 * q:SCALE_ROW0 + 4 * q + 4, :])
         with nc.allow_non_contiguous_dma(reason="one bias value a partition"):
             nc.sync.dma_start(out=bcol[:], in_=bias.rearrange("(j p) o -> p (j o)", p=P))
 
-        wbank = []
-        for l in range(3):
-            b = bank((4, 5, 7)[l])
+        for h in range(2):
+            spread = bank((4, 6)[h])
+            for c in range(2):
+                nc.tensor.transpose(spread[:, P * c:P * (c + 1)], wcol[0][:, 2 * h + c:2 * h + c + 1].to_broadcast([P, P]), ident[:])
+            nc.scalar.copy(out=wrow[:, HALF * h:HALF * (h + 1)].rearrange("p (n c) -> p n c", c=2),
+                           in_=spread[:, 0:HALF].rearrange("p (c n) -> p n c", c=2))
+        wbank = {}
+        for l in (1, 2):
+            wbank[l] = bank((5, 7)[l - 1])
             for c in range(4):
-                nc.tensor.transpose(b[:].rearrange("p (c n) -> p c n" if l == 0 else "p (n c) -> p c n", c=4)[:, c, :], wcol[l][:, c:c + 1].to_broadcast([P, P]), ident[:])
-            wbank.append(b)
-        nc.scalar.copy(out=wrow[:].rearrange("p (n c) -> p n c", c=4), in_=wbank[0][:].rearrange("p (c n) -> p n c", c=4))
+                nc.tensor.transpose(wbank[l][:].rearrange("p (n c) -> p c n", c=4)[:, c, :],
+                                    wcol[l][:, c:c + 1].to_broadcast([P, P]), ident[:])
 
         plain = {}
 
@@ -104,154 +114,141 @@ def tile_attend_threenn_kernel(tc, coarse, wa, wb, wc, wf, skip_words, skip_scal
                 nc.scalar.activation(out=g[:, e, :], in_=planes[2 * u + e][:].indirect(lists[l][:, 8 * c0:8 * (c0 + nch)]),
                                      func=ACT.Copy)
 
-        def interleave(n, tag):
-            grp[n] = sb([P, F, 4], BF16, tag)
-            for h in range(2):
-                nc.gpsimd.tensor_scalar(out=grp[n][:, 256 * h:256 * (h + 1), :], in0=raw[n][h][:].rearrange("p t f -> p f t"),
-                                        scalar1=1.0, scalar2=0.0, op0=ALU.mult, op1=ALU.add)
+        def interleave(n):
+            grouped[n] = laid.tile([P, F, 4], BF16, name="grouped_" + n, offset=4096 if n == "ws" else 4160, align_bytes=64)
+            nc.gpsimd.tensor_scalar(out=grouped[n][:].rearrange("p (a i) t -> p a t i", i=2),
+                                    in0=raw[n][:].rearrange("p t (a i) -> p a t i", i=2),
+                                    scalar1=1.0, scalar2=0.0, op0=ALU.mult, op1=ALU.add)
 
-        def quant_w(n, tag):
-            codes[n] = sb([P, F], U32, tag)
+        def quant_w(n, tile):
+            codes[n] = tile
             nc.vector.quantize_mx(out=codes[n][:].bitcast(FP8X4), scales=scal[n][:],
-                                  in_=grp[n][:].rearrange("p f t -> p (f t)"))
+                                  in_=grouped[n][:].rearrange("p f t -> p (f t)"))
 
-        def add_up(g, e, nch, ys, first, last):
+        def add_up(g, e, nch, sums, first, last):
             for c in range(nch):
-                col = 256 * (c % 2) + P * e
-                nc.tensor.matmul(ys[c // 2][:, col:col + P], g[:, P * c:P * (c + 1)], ident[:],
+                col = HALF * (c % 2) + P * e
+                nc.tensor.matmul(sums[c // 2][:, col:col + P], g[:, P * c:P * (c + 1)], ident[:],
                                  start=first and c % 2 == 0, stop=last and c % 2 == 1, is_transpose=True)
 
-        def fused(t, g):
-            nc.vector.tensor_tensor(g, planes[t][:].indirect(lists[0][:]), wrow[:], ALU.mult)
-
-        def weigh(u, l, c0, nch, ys, g, last):
+        def weigh(u, l, c0, nch, sums, g, last):
             n = P * nch
             nc.vector.tensor_tensor(g.rearrange("p (e n) -> p e n", e=2), plain[(u, l, c0)][:],
                                     wbank[l][:, P * c0:P * c0 + n].unsqueeze(1).to_broadcast([P, 2, n]), ALU.mult)
             for e in range(2):
-                add_up(g[:, n * e:n * (e + 1)], e, nch, ys, False, last and e == 1)
+                add_up(g[:, n * e:n * (e + 1)], e, nch, sums, False, last and e == 1)
 
-        def turn(y, nch, u, words, copy):
-            xb = words.bitcast(BF16).rearrange("i (c p e) -> i c p e", c=nch, e=2)
-            copy(out=xb, in_=y[:, 0:256 * nch].rearrange("i (c e p) -> i c p e", c=nch, e=2))
+        def round_pairs(sums, words, copy):
+            copy(out=words.bitcast(BF16).rearrange("i (c p e) -> i c p e", c=2, e=2),
+                 in_=sums[:, 0:2 * HALF].rearrange("i (c e p) -> i c p e", c=2, e=2))
 
-        def back(nch, u, zs, words):
-            for c in range(nch):
-                nc.tensor.transpose(zs[c][:, P * u:P * (u + 1)], words[:, P * c:P * (c + 1)], ident[:])
+        def turn_back(u, turned, words):
+            for c in range(2):
+                nc.tensor.transpose(turned[:, HALF * c + P * u:HALF * c + P * (u + 1)], words[:, P * c:P * (c + 1)], ident[:])
 
-        def weave(nch, z, words):
-            xg = words.bitcast(BF16)
-            nc.scalar.copy(out=words.rearrange("p (c i u) -> p c i u", c=nch, u=2),
-                           in_=z.rearrange("p (c u i) -> p c i u", c=nch, u=2))
-            return xg
+        def weave(turned, words):
+            nc.scalar.copy(out=words.rearrange("p (c i u) -> p c i u", c=2, u=2),
+                           in_=turned.rearrange("p (c u i) -> p c i u", c=2, u=2))
+            return words.bitcast(BF16)
 
-        def quant_x(name, nch, xg):
-            xc = sb([P, P * nch], U32, "xc" + name)
-            xs = sb([P, P * nch], U8, "xs" + name)
-            nc.vector.quantize_mx(out=xc[:].bitcast(FP8X4), scales=xs[:], in_=xg)
-            return xc, xs
+        def quant_x(name, woven):
+            x_codes = sb([P, HALF], U32, "xc" + name)
+            x_scales = sb([P, HALF], U8, "xs" + name)
+            nc.vector.quantize_mx(out=x_codes[:].bitcast(FP8X4), scales=x_scales[:], in_=woven)
+            return x_codes, x_scales
 
-        def product(dst, n, j, q, o, width, start, stop):
+        def product(dst, n, j, moving, start, stop):
             fc = slice(P * j, P * (j + 1))
             nc.tensor.matmul_mx(out=dst, lhsT=codes[n][:, fc].bitcast(FP8X4), lhsT_scale=scal[n][:, fc],
-                                rhs=q[0][:, o:o + width].bitcast(FP8X4 if n == "wf" else FP4X4),
-                                rhs_scale=q[1][:, o:o + width], start=start, stop=stop)
+                                rhs=moving[0][:, 0:HALF].bitcast(FP8X4 if n == "wf" else FP4X4),
+                                rhs_scale=moving[1][:, 0:HALF], start=start, stop=stop)
 
-        def relu(eng, dst, src, j):
-            bj = bcol[:, j:j + 1]
-            if eng == "s":
-                nc.scalar.activation(out=dst, in_=src, func=ACT.Relu, bias=bj)
-            else:
-                nc.vector.tensor_scalar(out=dst, in0=src, scalar1=bj, scalar2=0.0, op0=ALU.add, op1=ALU.max)
+        def product_pair(n, acc, j0, moving):
+            for jj in range(2):
+                product(acc[:, HALF * jj:HALF * (jj + 1)], n, j0 + jj, moving, n == "ws" and jj == 0, n == "wf" and jj == 1)
 
         oview = out.rearrange("(j p) i -> p j i", p=P)
 
-        obs = {}
+        def finish(src, h, j, on_scalar, queue):
+            o = buf(HALF, "o%d%d" % (h, j))
+            if on_scalar:
+                nc.scalar.activation(out=o, in_=src, func=ACT.Relu, bias=bcol[:, j:j + 1])
+            else:
+                nc.vector.tensor_scalar(out=o, in0=src, scalar1=bcol[:, j:j + 1], scalar2=0.0, op0=ALU.add, op1=ALU.max)
+            queue.dma_start(out=oview[:, j, HALF * h:HALF * (h + 1)], in_=o)
 
-        def products(n, h, half, q, o):
-            for jj in range(2):
-                product(obs[(h, half)][:, 256 * jj:256 * (jj + 1)], n, 2 * half + jj, q, o, 256,
-                        n == "ws" and jj == 0, n == "wf" and jj == 1)
+        skip = []
 
-        def finish(h, half, engine):
-            for jj in range(2):
-                j = 2 * half + jj
-                o = buf(256, "o%d%d" % (h, j))
-                relu(engine, o, obs[(h, half)][:, 256 * jj:256 * (jj + 1)], j)
-                queue = nc.scalar if (h, j) == (1, 1) else nc.sync
-                queue.dma_start(out=oview[:, j, 256 * h:256 * (h + 1)], in_=o)
-
-        def buf(n, tag):
-            return sb([P, n], F32, tag)[:]
+        def gather_words(h, tag):
+            g = sb([P, HALF], U16, tag)
+            nc.vector.tensor_copy(g[:], sk_w[:].indirect(lists[3][:, 16 * h:16 * (h + 1)]))
+            skip.append((g, sk_plane[:, HALF * h:HALF * (h + 1)]))
 
         gather_plain(0, 1, 0, 4, "wcol0")
         gather_plain(0, 2, 0, 4, "wcol1")
         gather_plain(1, 1, 0, 2, "wcol2")
-        gather_plain(1, 2, 0, 2, "pa")
-        gather_plain(1, 1, 2, 2, "pb")
-        gather_plain(1, 2, 2, 2, "pc")
+        gather_plain(1, 2, 0, 2, "plain_a3")
+        gather_plain(1, 1, 2, 2, "plain_b2")
+        gather_plain(1, 2, 2, 2, "plain_b3")
         first = buf(4 * NI, "first")
         for t in range(4):
-            fused(t, first[:, NI * t:NI * (t + 1)])
-        interleave("ws", "wrow")
-        y0 = [bank(0), bank(1)]
+            nc.vector.tensor_tensor(first[:, NI * t:NI * (t + 1)], planes[t][:].indirect(lists[0][:]), wrow[:], ALU.mult)
+        interleave("ws")
+
+        sums_lo = [bank(0), bank(1)]
         for e in range(2):
-            add_up(first[:, NI * e:NI * (e + 1)], e, 4, y0, e == 0, False)
-        weigh(0, 1, 0, 4, y0, buf(2 * NI, "plane0"), False)
-        weigh(0, 2, 0, 4, y0, buf(2 * NI, "plane1"), True)
-        ya, yb = [bank(2)], [bank(3)]
-        for h, y in enumerate((ya, yb)):
+            add_up(first[:, NI * e:NI * (e + 1)], e, 4, sums_lo, e == 0, False)
+        weigh(0, 1, 0, 4, sums_lo, buf(2 * NI, "plane0"), False)
+        weigh(0, 2, 0, 4, sums_lo, buf(2 * NI, "plane1"), True)
+        sums_hi = [bank(2), bank(3)]
+        for h in range(2):
             for e in range(2):
-                o = NI * (2 + e) + 256 * h
-                add_up(first[:, o:o + 256], e, 2, y, e == 0, False)
-        skip = []
+                o = NI * (2 + e) + HALF * h
+                add_up(first[:, o:o + HALF], e, 2, sums_hi[h:h + 1], e == 0, False)
 
-        def gather_words(h, tag):
-            g = sb([P, 256], U16, tag)
-            nc.vector.tensor_copy(g[:], sk_w[:].indirect(lists[3][:, 16 * h:16 * (h + 1)]))
-            skip.append((g, sk_plane[:, 256 * h:256 * (h + 1)]))
+        weigh(1, 1, 0, 2, sums_hi[0:1], buf(NI, "wcol0"), False)
+        gather_words(0, "wcol1")
+        weigh(1, 2, 0, 2, sums_hi[0:1], buf(NI, "wcol2"), True)
+        quant_w("ws", sb([P, F], U32, "plain_a3"))
+        interleave("wf")
+        acc_a = [bank(4), bank(6)]
+        for pair in range(2):
+            product_pair("ws", acc_a[pair], 2 * pair, skip[0])
 
-        gather_words(0, "wcol0")
-        weigh(1, 1, 0, 2, ya, buf(NI, "wcol1"), False)
-        quant_w("ws", "wcol2")
-        interleave("wf", "wrow")
-        obs[(0, 0)], obs[(0, 1)] = bank(4), bank(6)
-        products("ws", 0, 0, skip[0], 0)
-        products("ws", 0, 1, skip[0], 0)
-        weigh(1, 2, 0, 2, ya, buf(NI, "plane0"), True)
-        pairs = buf(4 * P, "plane2")
-        turn(y0[0], 2, 0, pairs[:, 0:256], nc.scalar.copy)
-        weigh(1, 1, 2, 2, yb, buf(NI, "plane1"), False)
-        weigh(1, 2, 2, 2, yb, buf(NI, "pa"), True)
-        gather_words(1, "pb")
-        turn(ya[0], 2, 1, pairs[:, 256:512], nc.scalar.copy)
-        za = bank(5)
-        back(2, 0, [za[:, 0:256], za[:, 256:512]], pairs[:, 0:256])
-        back(2, 1, [za[:, 0:256], za[:, 256:512]], pairs[:, 256:512])
-        pairs_b = [buf(2 * P, "plane3"), buf(2 * P, "pc")]
-        turn(y0[1], 2, 0, pairs_b[0], nc.scalar.copy)
-        turn(yb[0], 2, 1, pairs_b[1], nc.vector.tensor_copy)
-        xga = weave(2, za[:], buf(4 * P, "xga"))
-        quant_w("wf", "pa")
-        zb = bank(7)
-        back(2, 0, [zb[:, 0:256], zb[:, 256:512]], pairs_b[0])
-        back(2, 1, [zb[:, 0:256], zb[:, 256:512]], pairs_b[1])
-        obs[(1, 0)] = bank(3)
-        products("ws", 1, 0, skip[1], 0)
-        xqa = quant_x("a", 2, xga)
-        xgb = weave(2, zb[:], buf(4 * P, "xgb"))
-        products("wf", 0, 0, xqa, 0)
-        products("wf", 0, 1, xqa, 0)
-        xqb = quant_x("b", 2, xgb)
-        finish(0, 0, "s")
-        finish(0, 1, "v")
-        ends = {2: bank(5), 3: bank(7)}
+        late = laid.tile([P, 2 * NI], F32, name="late", offset=64, align_bytes=64)[:]
+        pairs_a = buf(2 * HALF, "plane2")
+        round_pairs(sums_lo[0], pairs_a[:, 0:HALF], nc.scalar.copy)
+        weigh(1, 1, 2, 2, sums_hi[1:2], late[:, 0:NI], False)
+        weigh(1, 2, 2, 2, sums_hi[1:2], late[:, NI:2 * NI], True)
+        gather_words(1, "plain_b2")
+        round_pairs(sums_hi[0], pairs_a[:, HALF:2 * HALF], nc.scalar.copy)
+        turned_a = bank(5)
+        for u in range(2):
+            turn_back(u, turned_a, pairs_a[:, HALF * u:HALF * (u + 1)])
+        pairs_b = [buf(HALF, "plane3"), buf(HALF, "plain_b3")]
+        round_pairs(sums_lo[1], pairs_b[0], nc.scalar.copy)
+        round_pairs(sums_hi[1], pairs_b[1], nc.scalar.copy)
+        woven_a = weave(turned_a[:], buf(2 * HALF, "woven_a"))
+        quant_w("wf", laid.tile([P, F], U32, name="codes_wf", offset=64 + 2048, align_bytes=64))
+        turned_b = bank(7)
+        for u in range(2):
+            turn_back(u, turned_b, pairs_b[u])
+
+        acc_b = bank(3)
+        product_pair("ws", acc_b, 0, skip[1])
+        x_a = quant_x("a", woven_a)
+        woven_b = weave(turned_b[:], buf(2 * HALF, "woven_b"))
+        for pair in range(2):
+            product_pair("wf", acc_a[pair], 2 * pair, x_a)
+        x_b = quant_x("b", woven_b)
+        for j in range(4):
+            finish(acc_a[j // 2][:, HALF * (j % 2):HALF * (j % 2 + 1)], 0, j, j < 2, nc.sync)
+        acc_end = {2: bank(5), 3: bank(7)}
         for j in (2, 3):
-            product(ends[j][:, 0:256], "ws", j, skip[1], 0, 256, True, False)
-        products("wf", 1, 0, xqb, 0)
-        finish(1, 0, "s")
+            product(acc_end[j][:, 0:HALF], "ws", j, skip[1], True, False)
+        product_pair("wf", acc_b, 0, x_b)
+        finish(acc_b[:, 0:HALF], 1, 0, True, nc.sync)
+        finish(acc_b[:, HALF:2 * HALF], 1, 1, True, nc.scalar)
         for j in (2, 3):
-            product(ends[j][:, 0:256], "wf", j, xqb, 0, 256, False, True)
-            o = buf(256, "o1%d" % j)
-            relu("v", o, ends[j][:, 0:256], j)
-            nc.sync.dma_start(out=oview[:, j, 256:512], in_=o)
+            product(acc_end[j][:, 0:HALF], "wf", j, x_b, False, True)
+            finish(acc_end[j][:, 0:HALF], 1, j, False, nc.sync)

@@ -18,6 +18,7 @@ P = 128
 K, U, R, T, NI, F = 512, 1024, 512, 2048, 512, 512
 HALF = 2 * P
 SCALE_ROW0 = P - 16
+WF_SPLIT = 5 * F // 8
 FLOPS = 2 * (K + R) * NI * F
 
 
@@ -114,10 +115,10 @@ def tile_attend_threenn_kernel(tc, coarse, wa, wb, wc, wf, skip_words, skip_scal
                 nc.scalar.activation(out=g[:, e, :], in_=planes[2 * u + e][:].indirect(lists[l][:, 8 * c0:8 * (c0 + nch)]),
                                      func=ACT.Copy)
 
-        def interleave(n):
+        def interleave(n, nf):
             grouped[n] = laid.tile([P, F, 4], BF16, name="grouped_" + n, offset=4096 if n == "ws" else 4160, align_bytes=64)
-            nc.gpsimd.tensor_scalar(out=grouped[n][:].rearrange("p (a i) t -> p a t i", i=2),
-                                    in0=raw[n][:].rearrange("p t (a i) -> p a t i", i=2),
+            nc.gpsimd.tensor_scalar(out=grouped[n][:, 0:nf, :].rearrange("p (a i) t -> p a t i", i=2),
+                                    in0=raw[n][:, :, 0:nf].rearrange("p t (a i) -> p a t i", i=2),
                                     scalar1=1.0, scalar2=0.0, op0=ALU.mult, op1=ALU.add)
 
         def quant_w(n, tile):
@@ -193,7 +194,7 @@ def tile_attend_threenn_kernel(tc, coarse, wa, wb, wc, wf, skip_words, skip_scal
         first = buf(4 * NI, "first")
         for t in range(4):
             nc.vector.tensor_tensor(first[:, NI * t:NI * (t + 1)], planes[t][:].indirect(lists[0][:]), wrow[:], ALU.mult)
-        interleave("ws")
+        interleave("ws", F)
 
         sums_lo = [bank(0), bank(1)]
         for e in range(2):
@@ -210,7 +211,7 @@ def tile_attend_threenn_kernel(tc, coarse, wa, wb, wc, wf, skip_words, skip_scal
         gather_words(0, "wcol1")
         weigh(1, 2, 0, 2, sums_hi[0:1], buf(NI, "wcol2"), True)
         quant_w("ws", sb([P, F], U32, "plain_a3"))
-        interleave("wf")
+        interleave("wf", WF_SPLIT)
         acc_a = [bank(4), bank(6)]
         for pair in range(2):
             product_pair("ws", acc_a[pair], 2 * pair, skip[0])
@@ -221,6 +222,7 @@ def tile_attend_threenn_kernel(tc, coarse, wa, wb, wc, wf, skip_words, skip_scal
         weigh(1, 1, 2, 2, sums_hi[1:2], late[:, 0:NI], False)
         weigh(1, 2, 2, 2, sums_hi[1:2], late[:, NI:2 * NI], True)
         gather_words(1, "plain_b2")
+        nc.vector.tensor_copy(out=grouped["wf"][:, WF_SPLIT:F, :], in_=raw["wf"][:, :, WF_SPLIT:F].rearrange("p t f -> p f t"))
         round_pairs(sums_hi[0], pairs_a[:, HALF:2 * HALF], nc.scalar.copy)
         turned_a = bank(5)
         for u in range(2):

from contextlib import ExitStack

import concourse.mybir as mybir
from concourse.masks import make_identity

F32 = mybir.dt.float32
BF16 = mybir.dt.bfloat16
I32 = mybir.dt.int32
U32 = mybir.dt.uint32
U16 = mybir.dt.uint16
U8 = mybir.dt.uint8
FP8X4 = mybir.dt.float8_e4m3fn_x4
FP4X4 = mybir.dt.float4_e2m1fn_x4
ACT = mybir.ActivationFunctionType
ALU = mybir.AluOpType

P = 128
K, U, R, T, NI, F = 512, 1024, 512, 2048, 512, 512
HALF = 2 * P
SCALE_ROW0 = P - 16
WF_SPLIT = 5 * F // 8
FLOPS = 2 * (K + R) * NI * F


def tile_attend_threenn_kernel(tc, coarse, wa, wb, wc, wf, skip_words, skip_scales, ws, bias,
                                    offs, offs2, offs3, offs4, out):
    nc = tc.nc
    with ExitStack() as ctx:
        keep = ctx.enter_context(tc.tile_pool(name="keep", bufs=1))
        laid = ctx.enter_context(tc.tile_pool(name="laid", bufs=1))
        psum = ctx.enter_context(tc.psum_pool(name="psum", bufs=1))
        made = []

        def sb(shape, dtype, tag):
            made.append(tag)
            return keep.tile(shape, dtype, name="%s_%d" % (tag, len(made)), tag=tag, align_bytes=64)

        def buf(n, tag):
            return sb([P, n], F32, tag)[:]

        def bank(b):
            made.append(b)
            return psum.tile([P, 512], F32, name="bank%d_%d" % (b, len(made)), tag="bank%d" % b)

        lists = [sb([P, NI // 16], U16, "list%d" % l) for l in range(4)]
        planes = [sb([P, U], F32, "plane%d" % t) for t in range(4)]
        wcol = [sb([P, 4], F32, "wcol%d" % l) for l in range(3)]
        bcol = sb([P, 4], F32, "bcol")
        ident = sb([P, P], F32, "ident")
        sk_w = sb([P, T], U16, "sk_w")
        sk_s = sb([P, T], U8, "sk_s")
        raw = {n: sb([P, 4, F], F32, "raw_" + n) for n in ("wf", "ws")}
        scal = {n: sb([P, F], U8, "scal_" + n) for n in ("wf", "ws")}
        grouped = {}
        codes = {}
        wrow = laid.tile([P, NI], F32, name="wrow", offset=4096, align_bytes=64)

        make_identity(nc, ident[:])
        sk_plane = sb([P, NI], U8, "sk_plane")
        nc.vector.memset(sk_s[:].bitcast(I32)[0:SCALE_ROW0, :], 0)
        nc.gpsimd.memset(sk_plane[:].bitcast(I32), 0)

        cview = coarse.rearrange("(p t) u -> p t u", t=4)
        wview = {"wf": wf.rearrange("(p t) f -> p t f", t=4), "ws": ws.rearrange("(p t) f -> p t f", t=4)}

        def load_matrix(n):
            nc.sync.dma_start(out=raw[n][:], in_=wview[n])

        def load_col(l):
            nc.sync.dma_start(out=wcol[l][:], in_=(wa, wb, wc)[l].rearrange("o (p c) -> p (o c)", c=4))

        with nc.allow_non_contiguous_dma(reason="two pairs of weights a partition"):
            nc.sync.dma_start(out=wcol[0][:].rearrange("p (h c) -> p h c", c=2), in_=wa.rearrange("o (h p c) -> p (o h) c", h=2, c=2))
        nc.sync.dma_start(out=sk_s[:].bitcast(I32)[SCALE_ROW0:P, :], in_=skip_scales[0].bitcast(I32))
        nc.sync.dma_start(lists[3][:], offs4)
        nc.sync.dma_start(out=planes[0][:], in_=cview[:, 0, :])
        nc.sync.dma_start(lists[0][:], offs)
        nc.sync.dma_start(lists[1][:], offs2)
        load_col(1)
        nc.sync.dma_start(out=planes[1][:], in_=cview[:, 1, :])
        load_col(2)
        nc.sync.dma_start(lists[2][:], offs3)
        for t in (2, 3):
            nc.sync.dma_start(out=planes[t][:], in_=cview[:, t, :])
        load_matrix("ws")
        nc.sync.dma_start(out=sk_w[:].bitcast(I32), in_=skip_words[0].bitcast(I32))
        picked = sb([P, NI], U8, "picked")
        nc.vector.tensor_copy(picked[:], sk_s[:].indirect(lists[3][:]))
        load_matrix("wf")

        for q in range(4):
            nc.gpsimd.dma_start(out=sk_plane[:].bitcast(I32)[32 * q:32 * q + 4, :],
                                in_=picked[:].bitcast(I32)[SCALE_ROW0 + 4 * q:SCALE_ROW0 + 4 * q + 4, :])
        with nc.allow_non_contiguous_dma(reason="one bias value a partition"):
            nc.sync.dma_start(out=bcol[:], in_=bias.rearrange("(j p) o -> p (j o)", p=P))

        for h in range(2):
            spread = bank((4, 6)[h])
            for c in range(2):
                nc.tensor.transpose(spread[:, P * c:P * (c + 1)], wcol[0][:, 2 * h + c:2 * h + c + 1].to_broadcast([P, P]), ident[:])
            nc.scalar.copy(out=wrow[:, HALF * h:HALF * (h + 1)].rearrange("p (n c) -> p n c", c=2),
                           in_=spread[:, 0:HALF].rearrange("p (c n) -> p n c", c=2))
        wbank = {}
        for l in (1, 2):
            wbank[l] = bank((5, 7)[l - 1])
            for c in range(4):
                nc.tensor.transpose(wbank[l][:].rearrange("p (n c) -> p c n", c=4)[:, c, :],
                                    wcol[l][:, c:c + 1].to_broadcast([P, P]), ident[:])

        plain = {}

        def gather_plain(u, l, c0, nch, tag):
            plain[(u, l, c0)] = g = sb([P, 2, P * nch], F32, tag)
            for e in range(2):
                nc.scalar.activation(out=g[:, e, :], in_=planes[2 * u + e][:].indirect(lists[l][:, 8 * c0:8 * (c0 + nch)]),
                                     func=ACT.Copy)

        def interleave(n, nf):
            grouped[n] = laid.tile([P, F, 4], BF16, name="grouped_" + n, offset=4096 if n == "ws" else 4160, align_bytes=64)
            nc.gpsimd.tensor_scalar(out=grouped[n][:, 0:nf, :].rearrange("p (a i) t -> p a t i", i=2),
                                    in0=raw[n][:, :, 0:nf].rearrange("p t (a i) -> p a t i", i=2),
                                    scalar1=1.0, scalar2=0.0, op0=ALU.mult, op1=ALU.add)

        def quant_w(n, tile):
            codes[n] = tile
            nc.vector.quantize_mx(out=codes[n][:].bitcast(FP8X4), scales=scal[n][:],
                                  in_=grouped[n][:].rearrange("p f t -> p (f t)"))

        def add_up(g, e, nch, sums, first, last):
            for c in range(nch):
                col = HALF * (c % 2) + P * e
                nc.tensor.matmul(sums[c // 2][:, col:col + P], g[:, P * c:P * (c + 1)], ident[:],
                                 start=first and c % 2 == 0, stop=last and c % 2 == 1, is_transpose=True)

        def weigh(u, l, c0, nch, sums, g, last):
            n = P * nch
            nc.vector.tensor_tensor(g.rearrange("p (e n) -> p e n", e=2), plain[(u, l, c0)][:],
                                    wbank[l][:, P * c0:P * c0 + n].unsqueeze(1).to_broadcast([P, 2, n]), ALU.mult)
            for e in range(2):
                add_up(g[:, n * e:n * (e + 1)], e, nch, sums, False, last and e == 1)

        def round_pairs(sums, words, copy):
            copy(out=words.bitcast(BF16).rearrange("i (c p e) -> i c p e", c=2, e=2),
                 in_=sums[:, 0:2 * HALF].rearrange("i (c e p) -> i c p e", c=2, e=2))

        def turn_back(u, turned, words):
            for c in range(2):
                nc.tensor.transpose(turned[:, HALF * c + P * u:HALF * c + P * (u + 1)], words[:, P * c:P * (c + 1)], ident[:])

        def weave(turned, words):
            nc.scalar.copy(out=words.rearrange("p (c i u) -> p c i u", c=2, u=2),
                           in_=turned.rearrange("p (c u i) -> p c i u", c=2, u=2))
            return words.bitcast(BF16)

        def quant_x(name, woven):
            x_codes = sb([P, HALF], U32, "xc" + name)
            x_scales = sb([P, HALF], U8, "xs" + name)
            nc.vector.quantize_mx(out=x_codes[:].bitcast(FP8X4), scales=x_scales[:], in_=woven)
            return x_codes, x_scales

        def product(dst, n, j, moving, start, stop):
            fc = slice(P * j, P * (j + 1))
            nc.tensor.matmul_mx(out=dst, lhsT=codes[n][:, fc].bitcast(FP8X4), lhsT_scale=scal[n][:, fc],
                                rhs=moving[0][:, 0:HALF].bitcast(FP8X4 if n == "wf" else FP4X4),
                                rhs_scale=moving[1][:, 0:HALF], start=start, stop=stop)

        def product_pair(n, acc, j0, moving):
            for jj in range(2):
                product(acc[:, HALF * jj:HALF * (jj + 1)], n, j0 + jj, moving, n == "ws" and jj == 0, n == "wf" and jj == 1)

        oview = out.rearrange("(j p) i -> p j i", p=P)

        def finish(src, h, j, on_scalar, queue):
            o = buf(HALF, "o%d%d" % (h, j))
            if on_scalar:
                nc.scalar.activation(out=o, in_=src, func=ACT.Relu, bias=bcol[:, j:j + 1])
            else:
                nc.vector.tensor_scalar(out=o, in0=src, scalar1=bcol[:, j:j + 1], scalar2=0.0, op0=ALU.add, op1=ALU.max)
            queue.dma_start(out=oview[:, j, HALF * h:HALF * (h + 1)], in_=o)

        skip = []

        def gather_words(h, tag):
            g = sb([P, HALF], U16, tag)
            nc.vector.tensor_copy(g[:], sk_w[:].indirect(lists[3][:, 16 * h:16 * (h + 1)]))
            skip.append((g, sk_plane[:, HALF * h:HALF * (h + 1)]))

        gather_plain(0, 1, 0, 4, "wcol0")
        gather_plain(0, 2, 0, 4, "wcol1")
        gather_plain(1, 1, 0, 2, "wcol2")
        gather_plain(1, 2, 0, 2, "plain_a3")
        gather_plain(1, 1, 2, 2, "plain_b2")
        gather_plain(1, 2, 2, 2, "plain_b3")
        first = buf(4 * NI, "first")
        for t in range(4):
            nc.vector.tensor_tensor(first[:, NI * t:NI * (t + 1)], planes[t][:].indirect(lists[0][:]), wrow[:], ALU.mult)
        interleave("ws", F)

        sums_lo = [bank(0), bank(1)]
        for e in range(2):
            add_up(first[:, NI * e:NI * (e + 1)], e, 4, sums_lo, e == 0, False)
        weigh(0, 1, 0, 4, sums_lo, buf(2 * NI, "plane0"), False)
        weigh(0, 2, 0, 4, sums_lo, buf(2 * NI, "plane1"), True)
        sums_hi = [bank(2), bank(3)]
        for h in range(2):
            for e in range(2):
                o = NI * (2 + e) + HALF * h
                add_up(first[:, o:o + HALF], e, 2, sums_hi[h:h + 1], e == 0, False)

        weigh(1, 1, 0, 2, sums_hi[0:1], buf(NI, "wcol0"), False)
        gather_words(0, "wcol1")
        weigh(1, 2, 0, 2, sums_hi[0:1], buf(NI, "wcol2"), True)
        quant_w("ws", sb([P, F], U32, "plain_a3"))
        interleave("wf", WF_SPLIT)
        acc_a = [bank(4), bank(6)]
        for pair in range(2):
            product_pair("ws", acc_a[pair], 2 * pair, skip[0])

        late = laid.tile([P, 2 * NI], F32, name="late", offset=64, align_bytes=64)[:]
        pairs_a = buf(2 * HALF, "plane2")
        round_pairs(sums_lo[0], pairs_a[:, 0:HALF], nc.scalar.copy)
        weigh(1, 1, 2, 2, sums_hi[1:2], late[:, 0:NI], False)
        weigh(1, 2, 2, 2, sums_hi[1:2], late[:, NI:2 * NI], True)
        gather_words(1, "plain_b2")
        nc.vector.tensor_copy(out=grouped["wf"][:, WF_SPLIT:F, :], in_=raw["wf"][:, :, WF_SPLIT:F].rearrange("p t f -> p f t"))
        round_pairs(sums_hi[0], pairs_a[:, HALF:2 * HALF], nc.scalar.copy)
        turned_a = bank(5)
        for u in range(2):
            turn_back(u, turned_a, pairs_a[:, HALF * u:HALF * (u + 1)])
        pairs_b = [buf(HALF, "plane3"), buf(HALF, "plain_b3")]
        round_pairs(sums_lo[1], pairs_b[0], nc.scalar.copy)
        round_pairs(sums_hi[1], pairs_b[1], nc.scalar.copy)
        woven_a = weave(turned_a[:], buf(2 * HALF, "woven_a"))
        quant_w("wf", laid.tile([P, F], U32, name="codes_wf", offset=64 + 2048, align_bytes=64))
        turned_b = bank(7)
        for u in range(2):
            turn_back(u, turned_b, pairs_b[u])

        acc_b = bank(3)
        product_pair("ws", acc_b, 0, skip[1])
        x_a = quant_x("a", woven_a)
        woven_b = weave(turned_b[:], buf(2 * HALF, "woven_b"))
        for pair in range(2):
            product_pair("wf", acc_a[pair], 2 * pair, x_a)
        x_b = quant_x("b", woven_b)
        for j in range(4):
            finish(acc_a[j // 2][:, HALF * (j % 2):HALF * (j % 2 + 1)], 0, j, j < 2, nc.sync)
        acc_end = {2: bank(5), 3: bank(7)}
        for j in (2, 3):
            product(acc_end[j][:, 0:HALF], "ws", j, skip[1], True, False)
        product_pair("wf", acc_b, 0, x_b)
        finish(acc_b[:, 0:HALF], 1, 0, True, nc.sync)
        finish(acc_b[:, HALF:2 * HALF], 1, 1, True, nc.scalar)
        for j in (2, 3):
            product(acc_end[j][:, 0:HALF], "wf", j, x_b, False, True)
            finish(acc_end[j][:, 0:HALF], 1, j, False, nc.sync)
